import numpy as np, ml_dtypes
CORES = [16,18,20,22]
N = 4
BF = ml_dtypes.bfloat16
V, M, E, RO, LINKS = 3584, 1792, 256, 3, 3
GR = np.arange(8)
def pairs(s):
    o = np.argsort(-s, axis=2, kind="stable")
    b = np.stack([np.sum(s > 15 - c, axis=2) for c in range(16)], 2) >> 1
    e = np.concatenate([b[:, :, 1:], np.full_like(b[:, :, :1], M)], 2)
    t = np.arange(M); j = np.sum(b[:, :, :, None] <= t, axis=2) - 1
    bt = np.take_along_axis(b, j, 2); h = np.take_along_axis(e, j, 2) - bt
    return np.take_along_axis(o, bt + t, 2), np.take_along_axis(o, bt + t + h, 2), t - bt, h
def pick(a, ix):
    return np.take_along_axis(a, ix[:, :, None, :], 3)
def swap(a):
    z = a.copy()
    for r in range(LINKS):
        q = (r + 1) % N
        z[r, ..., V - E:] = a[q, ..., :E]; z[q, ..., :E] = a[r, ..., V - E:]
    return z
def pool(rng, m):
    return np.stack([rng.choice(2 ** 20 - 1, m, replace=False) + 1 for g in range(8)])
def boards(rng):
    close = rng.choice(np.array([0, 60, 99, 100, 101, 190]), (N, 8, 1, V)) + (rng.random((N, 8, 16, V)) * rng.choice(np.array([1, 3, 8, 11]), (N, 8, 1, V))).astype(np.int64)
    return np.where(rng.random((N, 8, 1, V)) < 0.4, rng.integers(0, 201, (N, 8, 16, V)), close)
def scores(rng):
    w = rng.choice(np.array([0.5, 1.0, 2.0]), (N, 8, 1))
    return np.minimum((4 * rng.random((N, 8, V)) ** w).astype(np.int64), 3)
def clubs(rng, m):
    a = pool(rng, int(np.max(m)))
    n = a[GR[:, None], (rng.random((N, 8, V)) * m[:, None]).astype(np.int64)]
    p = a[GR[:, None, None], (rng.random((N, 8, 16, V)) * m[:, None, None]).astype(np.int64)]
    return n, np.where(np.arange(16)[:, None] < rng.integers(0, 25, (N, 8, 1, V)), p, 0)
def plant(rng, p, who, name, mask):
    w = np.ascontiguousarray(p).reshape(N, 8, 16 * V); ix = rng.integers(0, 16, who.shape) * V + who
    np.put_along_axis(w, ix, np.where(mask, name, np.take_along_axis(w, ix, 2)), 2)
    return w.reshape(N, 8, 16, V)
def pack(v, p, n, s):
    return {"x": np.ascontiguousarray(v.reshape(N, 128, V)).astype(np.float32).astype(BF), "hi": np.ascontiguousarray(p.reshape(N, 128, V)).astype(np.int32),
            "nm": np.ascontiguousarray(n).astype(np.int32), "sc": np.ascontiguousarray(s).astype(np.int32)}
def setup_inputs(rng):
    n, p = clubs(rng, rng.permutation(np.array([40, 80, 120, 160, 240, 320, 480, 640])))
    return pack(boards(rng), p, n, scores(rng))
def setup_inputs_ends(rng):
    q = V // 4
    cs = [(V, 0, 0, 0), (0, 0, V, 0), (1, 1, 1, V - 3), (V - 3, 1, 1, 1), (0, 1, V - 2, 1), (1, 0, V - 1, 0), (2, 0, V - 5, 3), (q + 1, q - 1, q + 1, q - 1),
          (0, 0, 0, V), (q + 1, 0, 0, V - q - 1), (0, V, 0, 0), (1, 0, 0, V - 1), (0, 0, 1, V - 1), (1, V - 2, 0, 1), (0, q - 1, 0, V - q + 1), (V - 3, 0, 0, 3)]
    s = np.zeros((N, 8, V), np.int64)
    for r in range(N):
        o = rng.permutation(16)[:8] if r > 1 else 8 * r + np.arange(8)
        for g in range(8): s[r, g] = rng.permutation(np.repeat(np.array([3, 2, 1, 0]), cs[int(o[g])]))
    n, p = clubs(rng, rng.permutation(np.array([40, 80, 120, 160, 240, 320, 480, 640])))
    return pack(boards(rng), p, n, s)
def setup_inputs_met(rng):
    s = scores(rng); a = pool(rng, N * V); n = np.ascontiguousarray(a.reshape(8, N, V).transpose(1, 0, 2))
    s[:2, 7] = rng.integers(0, 4, (2, 1))
    for r in (2, 3): s[r, 6] = rng.permutation(np.repeat(np.array([3, 2, 1, 0]), (4, 4, 4, V - 12)))
    p = a[GR[:, None, None], rng.integers(0, N * V, (N, 8, 16, V))]
    U, L, i, h = pairs(s); nu, nl = np.take_along_axis(n, U, 2), np.take_along_axis(n, L, 2)
    for r in (2, 3): p[r, 6][:, U[r, 6, 0:6:2]] = 0
    share = rng.choice(np.array([0.0, 0.02, 0.1, 0.3, 0.5, 0.9, 1.0]), (N, 8, 1)); share[0, :, 0] = (0.0, 0.02, 0.1, 0.3, 0.5, 0.7, 0.9, 1.0); share[1, 7] = 1.0
    again = (rng.random((N, 8, M)) < share) | ((i == h - 1) & (h % 2 == 1)); again[2:4, 6, :6] = np.arange(6) % 2 == 1
    p = plant(rng, p, L, nu, rng.random((N, 8, M)) < 0.3)
    p = plant(rng, p, U, np.roll(nl, -1, 2), rng.random((N, 8, M)) < 0.1)
    p = plant(rng, p, U, nl, again)
    return pack(boards(rng), p, n, s)
def setup_inputs_ties(rng):
    v = boards(rng); kind = rng.integers(0, 2, (N, 1, V)); row = np.arange(16)[:, None]
    v[:, 0] = 100
    v[:, 1] = np.where((row < 8) == (kind == 1), 150, 50)
    v[:, 2] = 200 * rng.integers(0, 2, (N, 16, V))
    v[:, 3] = 100 + (row == rng.integers(0, 16, (N, 1, V)))
    v[:, 4] = 100 + rng.integers(0, 2, (N, 16, V))
    v[:, 5] = np.where(kind == 1, 200, 0)
    n, p = clubs(rng, rng.permutation(np.array([40, 80, 120, 160, 240, 320, 480, 640])))
    s = scores(rng); s[:, 0] = np.where(np.arange(N)[:, None] % 2 == 0, rng.integers(0, 4, (N, 1)), s[:, 0])
    return pack(v, p, n, s)
def setup_inputs_alike(rng):
    n, p = clubs(rng, np.array([1, 1, 2, 3, 5, 17, 17, 400]))
    p[:, 1] = 0; p[:, 3] = 0; p[:, 5] = p[:, 5, :1].copy(); p[:, 6, :15] = 0
    n[:, 2] = np.where(rng.random((N, V)) < 0.5, 1, 2 ** 20 - 1); p[:, 2] = rng.choice(np.array([0, 1, 2 ** 20 - 1]), (N, 16, V))
    n[:, 3] = rng.integers(1, 4, (N, V))
    n[:, 7] = 2 ** 20 - 1 - rng.integers(0, 3, (N, V)); p[:, 7] = rng.integers(0, 3, (N, 16, V))
    return pack(boards(rng), p, n, scores(rng))
def setup_inputs_spread(rng):
    v = np.minimum((np.exp2(8 * rng.random((N, 8, 1, V))) * rng.random((N, 8, 16, V))).astype(np.int64), 200)
    n = np.minimum(np.exp2(20 * rng.random((N, 8, V))).astype(np.int64), 2 ** 20 - 1)
    p = np.minimum(np.exp2(20 * rng.random((N, 8, 16, V))).astype(np.int64), 2 ** 20 - 1) * (rng.random((N, 8, 16, V)) > 0.0625)
    n[:, 7] = 2 ** 20 - 1 - rng.integers(0, 200, (N, V)); p[:, 7] = 2 ** 20 - 1 - rng.integers(0, 200, (N, 16, V))
    return pack(v, p, n, np.minimum((4 * rng.random((N, 8, V)) ** 4).astype(np.int64), 3))
def check_inputs(d):
    bad = []
    for k, lo, hi_ in (("x", 0, 200), ("hi", 0, 2 ** 20 - 1), ("nm", 1, 2 ** 20 - 1), ("sc", 0, 3)):
        a = np.asarray(d[k]).astype(np.float64)
        if not np.all((a >= lo) & (a <= hi_)): bad.append("range of " + k)
        elif not np.all(a == np.floor(a)): bad.append("whole numbers in " + k)
    return bad
def reference(x, hi, nm, sc):
    v = x.astype(np.float32).astype(np.int32).reshape(N, 8, 16, V); p = hi.astype(np.int32).reshape(N, 8, 16, V)
    n = nm.astype(np.int32); s = sc.astype(np.int32)
    for rnd in range(RO):
        U, L, i, h = pairs(s)
        pu = pick(p, U)
        met = np.any(pu == np.take_along_axis(n, L, 2)[:, :, None, :], axis=2)
        ex = ((i & 1) == 0) & (i + 1 < h) & (met | np.roll(met, -1, 2))
        L = np.where(ex, np.roll(L, -1, 2), np.where(np.roll(ex, 1, 2), np.roll(L, 1, 2), L))
        xu, xl, pl = pick(v, U), pick(v, L), pick(p, L)
        nu, nl = np.take_along_axis(n, U, 2), np.take_along_axis(n, L, 2)
        wu, wl = np.sum(xu > xl, axis=2), np.sum(xl > xu, axis=2)
        su = np.take_along_axis(s, U, 2) + 2 * (wu > wl) + (wu == wl); sl = np.take_along_axis(s, L, 2) + 2 * (wl > wu) + (wu == wl)
        v = swap(np.concatenate([xu + (xl > xu), xl + (xu > xl)], 3))
        p = swap(np.concatenate([np.concatenate([nl[:, :, None, :], pu[:, :, :15]], 2), np.concatenate([nu[:, :, None, :], pl[:, :, :15]], 2)], 3))
        n = swap(np.concatenate([nu, nl], 2)); s = swap(np.concatenate([su, sl], 2))
    return {"yx": v.reshape(N, 128, V).astype(np.float32).astype(BF), "yn": n.astype(np.float32), "ys": s.astype(np.float32)}

@@ -1,0 +1,633 @@
+from concourse.bass import DstId, RemoteDMATransfer
+from concourse.mybir import AluOpType, ActivationFunctionType
+
+ALU, AF = AluOpType, ActivationFunctionType
+V, M, E, RO = 3584, 1792, 256, 3
+K = 224
+WID = 4096
+F, B, H, I, U16 = "float32", "bfloat16", "float16", "int32", "uint16"
+SCRATCH = {
+    "hint": ("sbuf", [128, V], I), "G0": ("sbuf", [128, WID], F), "G1": ("sbuf", [128, WID], F),
+    "N0": ("sbuf", [128, WID], F), "N1": ("sbuf", [128, WID], F), "X0": ("sbuf", [128, WID], B), "X1": ("sbuf", [128, WID], B),
+    "val": ("sbuf", [128, V], F), "winV": ("sbuf", [128, WID], F), "winA": ("sbuf", [128, WID], F),
+    "nl": ("sbuf", [128, M], F), "eq": ("sbuf", [128, M], B), "dd": ("sbuf", [128, M], B), "sg": ("sbuf", [128, M], B),
+    "gt": ("sbuf", [128, M], B), "nend": ("sbuf", [128, 2 * E], F), "nland": ("sbuf", [128, 2 * E], F),
+    "xend": ("sbuf", [128, E], B), "xland": ("sbuf", [128, 2 * E], B),
+    "sci": ("sbuf", [128, K], I), "nmi": ("sbuf", [128, K], I), "nmf": ("sbuf", [128, K], F),
+    "s": ("sbuf", [128, K], B), "sf": ("sbuf", [128, K], F), "mk": ("sbuf", [128, 8 * K], B), "q": ("sbuf", [128, 8 * K + 16], B),
+    "t1": ("sbuf", [128, 8 * K], H), "t2": ("sbuf", [128, 8 * K], H), "t3": ("sbuf", [128, 8 * K], B),
+    "bI": ("sbuf", [128, 32], I), "bF": ("sbuf", [128, 16], F), "par": ("sbuf", [128, 128], F),
+    "Ti": ("sbuf", [128, K], I), "Tj": ("sbuf", [128, K], I), "soff": ("sbuf", [128, K], U16),
+    "cV": ("sbuf", [128, 256], F), "cA": ("sbuf", [128, 256], F), "cS": ("sbuf", [128, K], F),
+    "off": ("sbuf", [128, K], U16), "off2": ("sbuf", [128, 112], U16),
+    "evI": ("sbuf", [128, 112], I), "evJ": ("sbuf", [128, 112], I), "Dp": ("sbuf", [128, 112], F), "fl": ("sbuf", [128, 112], F),
+    "pp": ("sbuf", [128, 112], F), "cl": ("sbuf", [128, K], B), "sk": ("sbuf", [128, K], B),
+    "so": ("sbuf", [128, RO * K], B), "soL": ("sbuf", [128, RO * K], B), "soR": ("sbuf", [128, RO * K], B),
+    "sE": ("sbuf", [128, RO * K], B), "sinL": ("sbuf", [128, RO * K], B), "sinR": ("sbuf", [128, RO * K], B),
+    "pidx": ("sbuf", [128, 4], I), "col": ("sbuf", [128, 16], F), "jt": ("sbuf", [128, 128], F), "kio": ("sbuf", [128, 256], F),
+    "rel": ("sbuf", [128, 128], B), "relj": ("sbuf", [128, 144], B), "ab": ("sbuf", [128, 3 * 128], B),
+    "a32": ("sbuf", [128, 144], B), "b32": ("sbuf", [128, 144], B), "sh": ("sbuf", [128, 6 * 128], B), "ta": ("sbuf", [128, 6 * 128], B),
+    "triL": ("sbuf", [128, 128], B), "triU": ("sbuf", [128, 128], B), "half": ("sbuf", [128, 128], B),
+    "ib": ("sbuf", [128, 128], B), "i16": ("sbuf", [128, 128], H), "i896": ("sbuf", [128, 128], B),
+    "i32": ("sbuf", [128, 128], F), "ineg": ("sbuf", [128, 128], B), "band": ("sbuf", [128, 4 * 128], F),
+    "Z": ("sbuf", [128, 144], B), "U": ("sbuf", [128, 144], B), "Yu": ("sbuf", [128, 144], B), "Yl": ("sbuf", [128, 144], B),
+    "Y": ("sbuf", [128, 144], B), "tau": ("sbuf", [128, K], H), "uu": ("sbuf", [128, 112], H), "keep": ("sbuf", [128, K], B),
+    "kt": ("sbuf", [128, K], F), "ones": ("sbuf", [128, K], B), "cst": ("sbuf", [128, 96], B), "zero": ("sbuf", [128, 256], F),
+    "pS": ("psum", [128, 512], F), "pT": ("psum", [128, 512], F), "pA": ("psum", [128, 512], F), "pL": ("psum", [128, 512], F),
+    "pO": ("psum", [128, 512], F), "pW": ("psum", [128, 512], F), "pX0": ("psum", [128, 512], F), "pX1": ("psum", [128, 512], F),
+}
+NDMA = 100
+SEMAPHORES = (["eV", "eA", "eP", "eG"] + ["d%d" % i for i in range(NDMA)]
+              + ["%s%d" % (k, r) for k in ("aS", "aO", "aN", "aM", "aG", "aX") for r in range(RO)])
+KA = (146, 114, 118)
+SHIFTS = (14, 15, -14, -15, -1, 1)
+QUARTERS = ((1536, M), (0, 512), (512, 1024), (1024, 1536))
+BIG = 1 << 20
+
+
+def rank_program(g, core, T, topo):
+    rank = T.rank_of(core)
+    if rank is None:
+        return
+    nr = len(T.cores)
+    left = T.cores[rank - 1] if rank > 0 else None
+    right = T.cores[rank + 1] if rank + 1 < nr else None
+
+    def ext_first(r):
+        return V
+
+    def ext_last(r):
+        return V + (E if r > 0 else 0)
+
+    wid = V + (E if left is not None else 0) + (E if right is not None else 0)
+    lo = E if left is not None else 0
+    hi = V - E if right is not None else V
+    Q = {"V": g.vector, "A": g.scalar, "P": g.tensor, "S": g.sync, "G": g}
+    ops = []
+
+    def v(name, a=None, b=None, st=None):
+        if a is None:
+            return (T[name][:], [(name, 0, BIG)])
+        if st is None:
+            return (T[name][:, a:b], [(name, a, b)])
+        return (T[name][:, a:b:st], [(name, a, b)])
+
+    def ve(name, a):
+        return v(name, a, a + E)
+
+    def c(name, j):
+        return v(name, j, j + 1)
+
+    def w(name, o):
+        return v(name, o, o + 128)
+
+    def shift(s, name="sh"):
+        return w(name, 128 * SHIFTS.index(s))
+
+    def row(name, r, a, b):
+        return (T[name][r::16, a:b], [(name, a, b)])
+
+    def ind(name, n, offs, a, b):
+        return (T[name][:, 0:n].indirect(T[offs][:, a:b]), [(name, 0, n), (offs, a, b)])
+
+    def blk(name, b, o=0, n=1):
+        return v(name, o + b * K, o + (b + n) * K)
+
+    def ap(x):
+        return x[0] if isinstance(x, tuple) else x
+
+    def regs(*xs):
+        out = []
+        for x in xs:
+            if isinstance(x, tuple):
+                out += x[1]
+        return out
+
+    def add(eng, kind, fn, R, W, n=1, sem=None):
+        ops.append({"eng": eng, "kind": kind, "fn": fn, "R": R, "W": W, "n": n, "sem": sem})
+
+    def ts(out, in0, s1, op0, s2=None, op1=None):
+        if op1 is None:
+            add("V", "c", lambda: g.vector.tensor_scalar(out[0], in0[0], ap(s1), None, op0), regs(in0, s1), out[1])
+        else:
+            add("V", "c", lambda: g.vector.tensor_scalar(out[0], in0[0], ap(s1), ap(s2), op0, op1), regs(in0, s1, s2), out[1])
+
+    def tt(out, a, b, op):
+        add("V", "c", lambda: g.vector.tensor_tensor(out[0], a[0], b[0], op), regs(a, b), out[1])
+
+    def cp(out, a):
+        add("V", "c", lambda: g.vector.tensor_copy(out[0], a[0]), regs(a) + out[1][1:], out[1][:1])
+
+    def ms(out, x):
+        add("V", "c", lambda: g.vector.memset(out[0], x), [], out[1])
+
+    def scan(out, a):
+        add("V", "c", lambda: g.vector.tensor_tensor_scan(out[0], a[0], a[0], 0.0, ALU.add, ALU.max), a[1], out[1])
+
+    def act(out, a, func, bias=0.0, scale=1.0):
+        if bias == 0.0 and scale == 1.0:
+            add("A", "c", lambda: g.scalar.activation(out[0], a[0], func), regs(a) + out[1][1:], out[1][:1])
+        else:
+            add("A", "c", lambda: g.scalar.activation(out[0], a[0], func, bias=ap(bias), scale=ap(scale)),
+                regs(a, bias, scale) + out[1][1:], out[1][:1])
+
+    def gat(eng, out, a):
+        if eng == "V":
+            cp(out, a)
+        else:
+            act(out, a, AF.Identity)
+
+    def mm(out, l, r, start=False, stop=False):
+        add("P", "c", lambda: g.tensor.matmul(out[0], l[0], r[0], start, stop), regs(l, r), out[1])
+
+    def iota(out, pat, base, cm, flag=True):
+        if flag:
+            add("G", "c", lambda: g.iota(out[0], pat, base, cm, allow_small_or_imprecise_dtypes=True), [], out[1])
+        else:
+            add("G", "c", lambda: g.iota(out[0], pat, base, cm), [], out[1])
+
+    def dma(eng, pairs, accum=False):
+        def fn(sem):
+            for o, i in pairs:
+                if accum:
+                    g.dma_start(o[0], i[0], accum_op=ALU.add).then_inc(sem, 16)
+                else:
+                    Q[eng].dma_start(o[0], i[0]).then_inc(sem, 16)
+        R, W = [], []
+        for o, i in pairs:
+            R += i[1]
+            W += o[1]
+        add(eng, "d", fn, R, W, 16 * len(pairs))
+
+    def half_mask(src, dst):
+        en = topo.engines(src, dst)
+        h = len(en) // 2
+        part = en[h:] if T.rank_of(dst) > T.rank_of(src) else en[:h]
+        return sum(1 << e for e in part), len(part)
+
+    def send(sem, to_left, to_right):
+        tr, R, cnt = [], [], 0
+        for dst, x in ((left, to_left), (right, to_right)):
+            if dst is None or x is None:
+                continue
+            rid, pid, _se = topo.addr(dst)
+            mask, k = half_mask(core, dst)
+            tr.append(RemoteDMATransfer(dst_ids=[DstId(rid=rid, pnc=pid)], dma_engine_mask=mask, remote_sem=T.sem[sem],
+                                        src=x[0][0], dst=x[1][0]))
+            R += x[0][1]
+            cnt += k
+        if tr:
+            add("G", "d", lambda s: g.remote_dma_fused(tr, local_sem=s), R, [], cnt)
+
+    def recv(sem, from_left, from_right):
+        W, cnt = [], 0
+        for src, x in ((left, from_left), (right, from_right)):
+            if src is None or x is None:
+                continue
+            W += x[1]
+            cnt += half_mask(src, core)[1]
+        if cnt:
+            add(None, "r", None, [], W, cnt, sem)
+
+    def swap_ends(sem, name):
+        send(sem, (ve(name, 0), ve(name, ext_last(rank - 1))), (ve(name, V - E), ve(name, ext_first(rank + 1))))
+        recv(sem, ve(name, ext_first(rank)), ve(name, ext_last(rank)))
+
+    def both(sem, src, at_left, at_right):
+        send(sem, (src, at_right), (src, at_left))
+        recv(sem, at_left, at_right)
+
+    IB = v("ib")
+    dma("S", [(v("sci"), v("sc"))])
+    dma("S", [(v("nmi"), v("nm"))])
+    iota(c("pidx", 0), [[0, 1]], 0, 1, False)
+    iota(v("jt"), [[64, 8], [1, 16]], 0, 0)
+    iota(v("kio"), [[1, 256]], 0, 0)
+    iota(v("val", 0, 16 * KA[0]), [[1, KA[0]], [K, 16]], 64, 0)
+    iota(v("val", 16 * KA[0], V), [[1, K - KA[0]], [K, 16]], 64 + KA[0], 0)
+    ms(v("zero"), 0.0)
+    dma("S", [(row("winA", 0, 0, WID), v("zero")), (row("winV", 0, 0, WID), v("zero"))])
+    dma("S", [(v("hint", 0, M), v("hi", 0, M))])
+    ts(c("pidx", 1), c("pidx", 0), 15, ALU.bitwise_and)
+    ts(c("pidx", 2), c("pidx", 0), 4, ALU.logical_shift_right)
+    ms(v("cst", 0, 16), -1792.0)
+    cp(c("col", 0), c("pidx", 1))
+    ts(c("col", 1), c("pidx", 2), -64.0, ALU.mult)
+    ms(v("cst", 16, 48), -0.25)
+    tt(c("col", 2), c("col", 0), c("col", 1), ALU.subtract)
+    ms(v("cst", 48, 64), -1.0)
+    ts(v("rel"), v("jt"), c("col", 2), ALU.subtract)
+    ms(v("cst", 64, 80), 0.0)
+    ms(v("cst", 80, 96), 1792.0)
+    ms(v("q", 0, 16), 0.0)
+    for j, bias in enumerate((0.0, -8.0, 8.0)):
+        act(w("ab", 128 * j), v("rel"), AF.Abs, bias=bias)
+    ts(IB, v("rel"), 0.0, ALU.is_equal)
+    ts(v("i16"), v("rel"), 0.0, ALU.is_equal)
+    ts(v("half"), w("ab", 0), 15.5, ALU.is_lt, 0.5, ALU.mult)
+    ts(v("triL"), w("ab", 128), 7.5, ALU.is_lt)
+    ts(v("triU"), w("ab", 256), 7.5, ALU.is_lt)
+    cp(v("s"), v("sci"))
+    act(v("i896"), IB, AF.Silu, scale=896.0)
+    act(c("col", 9), c("col", 1), AF.Identity, bias=-16.0, scale=0.25)
+    act(c("col", 7), c("col", 0), AF.Identity, bias=-(lo + hi - 1) / 2.0, scale=224.0)
+    act(c("col", 8), c("col", 0), AF.Sign, bias=-7.5)
+    act(c("col", 4), c("col", 0), AF.Identity, bias=-896.0 - 895.75, scale=224.0)
+    act(c("col", 6), c("col", 0), AF.Identity, bias=1.0)
+    act(v("relj"), v("kio", 0, 144), AF.Identity, bias=c("col", 9))
+    act(c("col", 5), c("col", 8), AF.Identity, bias=c("col", 4), scale=-895.75)
+    act(v("a32"), v("relj"), AF.Abs, bias=0.5)
+    act(v("b32"), v("relj"), AF.Abs)
+    act(v("Z"), v("a32"), AF.Relu, bias=1.5, scale=-1.0)
+    act(v("U"), v("b32"), AF.Relu, bias=1.0, scale=-1.0)
+    act(v("a32"), v("relj"), AF.Abs, bias=-8.0)
+    act(v("Yu"), v("U"), AF.Identity, scale=-1.0)
+    act(v("Yl"), v("a32"), AF.Relu, bias=1.0, scale=-1.0)
+
+    def more_constants(step):
+        if step == 0:
+            for s in SHIFTS:
+                act(shift(s, "ta"), v("rel"), AF.Abs, bias=float(-s))
+            act(v("sh"), v("ta"), AF.Relu, bias=1.0, scale=-1.0)
+        else:
+            act(v("kt"), v("kio", 0, K), AF.Abs, bias=c("col", 7))
+            act(v("ones"), v("kio", 0, K), AF.Identity, bias=1.0, scale=0.0)
+            act(v("kt"), v("kt"), AF.Sign, bias=(hi - lo) / 2.0, scale=-1.0)
+            act(v("i32"), IB, AF.Identity)
+            act(v("keep"), v("kt"), AF.Relu)
+            act(w("band", 128), shift(15), AF.Identity)
+            act(w("band", 384), shift(-15), AF.Identity, scale=-1.0)
+            act(v("ineg"), IB, AF.Identity, scale=-1.0)
+            for a in ([0] if left is not None else []) + ([V - E] if right is not None else []):
+                act(ve("N1", a), v("zero"), AF.Identity)
+
+    def x_lower(X, a, b, eng, with_gt, bank):
+        px = v(bank, 0, b - a)
+        mm(px, IB, v(X, a, b), True)
+        mm(px, IB, v("dd", a, b))
+        if with_gt:
+            mm(px, IB, v("gt", a, b))
+        mm(px, v("ineg"), v("sg", a, b), False, True)
+        return lambda: gat(eng, v(X, M + a, M + b), px)
+
+    def from_ends(at_left, at_right, o, stop):
+        arr = []
+        if right is not None:
+            arr += [(192, K, 14, v(at_right, o, o + 32)), (0, 192, 15, v(at_right, o + 32, o + K))]
+        if left is not None:
+            arr += [(0, 32, -14, v(at_left, o + 192, o + K)), (32, K, -15, v(at_left, o, o + 192))]
+        for j, (a, b, s, src) in enumerate(arr):
+            mm(v("pS", a, b), shift(s), src, False, stop and j == len(arr) - 1)
+
+    for r in range(RO):
+        C = 4 + 2 * r
+        n = V if r == 0 else wid
+        Gc, Nc, Xc = "G%d" % (r % 2), "N%d" % (r % 2), "X%d" % (r % 2)
+        Gn, Nn, Xn = "G%d" % (1 - r % 2), "N%d" % (1 - r % 2), "X%d" % (1 - r % 2)
+        last = r == RO - 1
+        ka = KA[r]
+        mm(v("pS", 0, 48), IB, v("cst", 0, 48), True)
+        mm(v("pS", 0, 48), IB, v("cst", 48, 96))
+        uppers = []
+        if r > 0:
+            for (a, b), bank in zip(QUARTERS, ("pX0", "pX1", "pA", "pL")):
+                mm(v(bank, 0, b - a), IB, v(Xc, a, b), True)
+                mm(v(bank, 0, b - a), IB, v("gt", a, b), False, True)
+                uppers.append(lambda o=v(Xc, a, b), i=v(bank, 0, b - a): gat("A", o, i))
+        for b in range(C):
+            ts(blk("mk", b), v("s"), float(C - 1 - b), ALU.is_equal)
+        scan(v("q", 16, 16 + C * K), v("mk", 0, C * K))
+        e_all = v("q", 15, 16 + C * K, K)
+        mm(v("pS", 16, 17 + C), v("half"), e_all)
+        mm(v("pS", 32, 33 + C), v("half"), e_all)
+        mm(v("pS", 0, C), v("triL"), v("q", 15 + K, 16 + C * K, K))
+        mm(v("pS", 0, C), v("triU"), v("q", 15, 16 + (C - 1) * K, K), False, True)
+
+        def member(b, m=1):
+            tt(blk("t3", b, 0, m), blk("mk", b, 0, m), blk("q", b, 16, m), ALU.mult)
+            for j in range(b, b + m):
+                mm(v("pT", 0, K), IB, blk("t3", j), j == 0)
+
+        def base(b):
+            ts(blk("t1", b), blk("mk", b), c("par", b), ALU.mult)
+            mm(v("pT", 0, K), v("i16"), blk("t1", b))
+
+        def floats(b):
+            act(blk("q", b, 16), blk("t3", b), AF.Sign, bias=c("par", 80 + b), scale=-1.0)
+            mm(v("pT", 0, K), v("i896"), blk("q", b, 16))
+
+        if r == 0:
+            cp(v("nmf"), v("nmi"))
+            dma("S", [(row("N0", 0, 0, V), v("nmf"))])
+            dma("S", [(v("hint", M, V), v("hi", M, V))])
+            dma("S", [(row("N0", j, 0, V), row("N0", 0, 0, V)) for j in range(1, 16)])
+        member(0, 2)
+        cp(v("bI"), v("pS", 16, 48))
+        member(2)
+        tt(v("par", 0, C), v("pS", 0, C), v("bI", 0, C), ALU.subtract)
+        tt(v("par", 16, 16 + C), v("bI", 16, 16 + C), v("bI", 1, 1 + C), ALU.subtract)
+        tt(v("par", 32, 32 + C), v("bI", 1, 1 + C), v("par", 0, C), ALU.subtract)
+        base(0)
+        tt(v("par", 64, 64 + C), v("par", 32, 32 + C), v("par", 16, 16 + C), ALU.subtract)
+        ts(v("par", 48, 48 + C), v("par", 32, 32 + C), -1792.5, ALU.add, 0.5, ALU.max)
+        ts(v("par", 80, 80 + C), v("par", 64, 64 + C), -0.5, ALU.add, 0.5, ALU.max)
+        base(1)
+        for b in range(3, C):
+            member(b)
+            base(b - 1)
+            floats(b - 3)
+        base(C - 1)
+        floats(C - 3)
+        floats(C - 2)
+        for b in range(C):
+            ts(blk("t2", b), blk("t3", b), c("par", 48 + b), ALU.is_gt, c("par", 16 + b), ALU.mult)
+        for b in range(C):
+            mm(v("pT", 0, K), v("i16"), blk("t2", b), False, b == C - 1)
+        for put in uppers:
+            put()
+        ts(v("par", 96, 97 + C), v("pS", 16, 17 + C), -896.0, ALU.add)
+        cp(v("bF"), v("bI", 0, 16))
+        if r == 0:
+            more_constants(0)
+        ts(v("Ti"), v("pT", 0, K), float(1792 - 896 * (C - 1)), ALU.add, 4097.0, ALU.mult)
+        for a, b in ((0, ka), (ka, K)):
+            ts(v("Tj", a, b), v("Ti", a, b), 4, ALU.logical_shift_right, 4095, ALU.bitwise_and)
+        for a, b in ((0, ka), (ka, K)):
+            cp(v("soff", a, b), v("Tj", a, b))
+        act(ind("winA", WID, "soff", 0, ka), v("val", 0, 16 * ka), AF.Silu)
+        dma("A", [(v("cA"), row("winA", 0, 0, WID))])
+        cp(ind("winV", WID, "soff", ka, K), v("val", 16 * ka, V))
+        dma("S", [(v("cV"), row("winV", 0, 0, WID))])
+        if r == 0:
+            dma("A", [(v("X0", 0, V), v("x"))])
+            more_constants(1)
+            ts(v("tau"), v("kio", 0, K), c("col", 5), ALU.add)
+            ts(v("uu"), v("kio", 0, 112), 16.0, ALU.mult, c("col", 6), ALU.add)
+            tt(v("Y"), v("Yu"), v("Yl"), ALU.add)
+            tt(w("band", 0), shift(-1), IB, ALU.subtract)
+            tt(w("band", 256), IB, shift(1), ALU.subtract)
+            cp(v("G0", 0, V), v("hint"))
+            if left is not None:
+                iota(v("val", 0, V, 16), [[1, K]], 64 + ext_first(rank), 0)
+                iota(v("val", 1, 16 * 32, 16), [[1, 32]], 64 + ext_first(rank) + K, 0)
+            if right is not None:
+                iota(v("val", 16 * 192 + 14, V, 16), [[1, 32]], 64 + ext_last(rank), 0)
+                iota(v("val", 15, V, 16), [[1, K]], 64 + ext_last(rank) + 32, 0)
+        else:
+            puts = [x_lower(Xc, a, b, "A", False, bank) for (a, b), bank in zip(QUARTERS, ("pX0", "pX1", "pW", "pL"))]
+            puts[0]()
+            swap_ends("aX%d" % (r - 1), Xc)
+            for put in puts[1:]:
+                put()
+        for b in range(1, C):
+            ts(blk("mk", b), v("tau"), c("par", 96 + b), ALU.is_lt)
+        for b in range(1, C + 1):
+            ts(v("t1", 112 * b, 112 * b + 112), v("uu"), c("bF", b), ALU.is_ge, c("par", 15 + b), ALU.mult)
+        mm(v("pO", 0, K), IB, v("ones"), True)
+        for b in range(1, C):
+            mm(v("pO", 0, K), IB, blk("mk", b), False, b == C - 1)
+        mm(v("pS", 64, 176), v("i16"), v("uu"), True)
+        for b in range(1, C + 1):
+            mm(v("pS", 64, 176), v("i16"), v("t1", 112 * b, 112 * b + 112), False, b == C)
+        cp(blk("so", r), v("pO", 0, K))
+        both("aO%d" % r, blk("so", r), blk("soL", r), blk("soR", r))
+        cp(v("evI"), v("pS", 64, 176))
+        tt(v("sk"), blk("so", r), v("keep"), ALU.mult)
+        ts(v("evJ"), v("evI"), 1, ALU.bitwise_and)
+        tt(v("cS", 112, K), v("cV", 112, K), v("cA", 112, K), ALU.add)
+        tt(v("cS", 0, 112), v("cV", 0, 112), v("cA", 0, 112), ALU.add)
+        ts(v("off", 112, K), v("cS", 112, K), -63.75, ALU.add)
+        ts(v("off", 0, 112), v("cS", 0, 112), -63.75, ALU.add)
+        if not last:
+            dma("S", [(row("winA", 0, 0, WID), v("zero")), (row("winV", 0, 0, WID), v("zero"))])
+        mm(v("pA", 128, 240), w("band", 0), v("cS", 112, K), True)
+        mm(v("pA", 128, 239), w("band", 128), v("cS", 113, K), False, True)
+        mm(v("pL", 0, 112), v("i32"), v("cS", 112, K), True)
+        mm(v("pS", 0, K), IB, v("sk"), True)
+
+        def met(a, b):
+            for i in range(16):
+                mm(v("pA", a, b), w("Z" if i else "U", 16 - i), v("eq", 16 * a + i, 16 * b, 16), i == 0)
+            e = min(b, 111)
+            mm(v("pA", a, e), w("U", 1), v("eq", 16 * a + 16, 16 * e + 1, 16), False, True)
+
+        for j in range(7):
+            gat("A", ve("nl", E * j), ind(Nc, n, "off", 112 + 16 * j, 128 + 16 * j))
+        for j in range(7):
+            tt(ve("eq", E * j), ind(Gc, n, "off", 16 * j, 16 * j + 16), ve("nl", E * j), ALU.is_equal)
+            if j == 0:
+                tt(v("Dp"), v("pA", 128, 240), v("evJ"), ALU.mult)
+            if j == 3:
+                met(0, 63)
+        met(63, 112)
+        if not last:
+            dma("S", [(row(Gc, 15 - r, 0, n), row(Nc, 0, 0, n))])
+        for a, b in ((0, 16), (96, 112), (16, 56), (56, 96)):
+            gat("A", v(Xn, 16 * a, 16 * b), ind(Xc, n, "off", a, b))
+        if last:
+            land_first, land_last = (lambda k: ve("nland", 0)), (lambda k: ve("nland", E))
+            dma("S", [(v("yx", lo, 1024), v(Xn, lo, 1024)), (v("yx", 1536, M), v(Xn, 1536, M))])
+        else:
+            land_first, land_last = (lambda k, x=Nn: ve(x, ext_first(k))), (lambda k, x=Nn: ve(x, ext_last(k)))
+        if left is not None:
+            gat("V", ve("nend", 0), ind(Nc, n, "off", 0, 16))
+            send("aN%d" % r, (ve("nend", 0), land_last(rank - 1)), None)
+        recv("aN%d" % r, None, land_last(rank))
+        ts(v("fl"), v("pA", 0, 112), 0.5, ALU.is_gt)
+        tt(v("pp"), v("fl"), v("Dp"), ALU.mult)
+        mm(v("pL", 0, 112), w("band", 256), v("pp"))
+        mm(v("pL", 1, 112), w("band", 384), v("pp", 0, 111), False, True)
+        ts(v("off2"), v("pL", 0, 112), -63.75, ALU.add)
+        from_ends("soL", "soR", r * K, False)
+
+        def diff(a, b):
+            tt(v("dd", 16 * a, 16 * b), ind(Xc, n, "off2", a, b), v(Xn, 16 * a, 16 * b), ALU.subtract)
+
+        def sign(a, b, eng):
+            if eng == "V":
+                ts(v("sg", 16 * a, 16 * b), v("dd", 16 * a, 16 * b), 1.0, ALU.min, -1.0, ALU.max)
+            else:
+                act(v("sg", 16 * a, 16 * b), v("dd", 16 * a, 16 * b), AF.Sign)
+
+        def greater(a, b):
+            ts(v("gt", 16 * a, 16 * b), v("dd", 16 * a, 16 * b), 0.5, ALU.is_gt)
+
+        def wins(i, a, b, name, start=False, stop=False, bank="pW"):
+            mm(v(bank, a, b), w(name, 16 - i), v("sg", K * i + a, K * i + b), start, stop)
+
+        def names(eng, offs, a, b):
+            o = M if offs == "off2" else 0
+            gat(eng, v(Gn, o + 16 * a, o + 16 * b), ind(Nc if last else Gc, n, offs, a, b))
+
+        def last_names():
+            if right is not None:
+                send("aM%d" % r, None, (ve("nend", E), land_first(rank + 1)))
+            recv("aM%d" % r, land_first(rank), None)
+
+        def end_results():
+            act(blk("sE", r), v("pT", 0, K), AF.Sign)
+            both("aS%d" % r, blk("sE", r), blk("sinL", r), blk("sinR", r))
+            yf = "Y" if left is None else "Yl"
+            yl = "Y" if right is None else "Yu"
+            wins(0, 0, K, yf, True)
+            wins(1, 0, 32, yf)
+            wins(6, 192, K, yl)
+            wins(7, 0, K, yl)
+
+        if right is not None:
+            gat("A", ve("nend", E), ind(Nc, n, "off2", 96, 112))
+        if last:
+            last_names()
+        diff(0, 16)
+        diff(96, 112)
+        sign(0, 16, "V")
+        sign(96, 112, "V")
+        wins(0, 0, K, "Yu", True, bank="pT")
+        wins(1, 0, 32, "Yu", bank="pT")
+        wins(6, 192, K, "Yl", bank="pT")
+        wins(7, 0, K, "Yl", False, True, bank="pT")
+        if not last:
+            names("A", "off", 0, 16)
+            end_results()
+            last_names()
+            for a, b in ((16, 42), (42, 56), (56, 70), (70, 84), (84, 96)):
+                diff(a, b)
+                sign(a, b, "A")
+            wins(1, 32, K, "Y")
+            for i in (2, 3, 4, 5):
+                wins(i, 0, K, "Y")
+            wins(6, 0, 192, "Y", False, True)
+            from_ends("sinL", "sinR", r * K, True)
+            greater(0, 56)
+            ts(v("cl"), v("pW", 0, K), 1.0, ALU.min, -1.0, ALU.max)
+            greater(56, 112)
+            tt(v("s"), v("pS", 0, K), v("cl"), ALU.add)
+            names("A", "off2", 0, 112)
+            names("A", "off", 16, 112)
+            dma("S", [(row(Nn, 0, 0, V), row(Gn, 15 - r, 0, V))])
+            dma("S", [(row(Gn, 15 - r, 0, M), row(Nn, 0, M, V)), (row(Gn, 15 - r, M, V), row(Nn, 0, 0, M))])
+            dma("S", [(row(Nn, j, lo, hi), row(Nn, 0, lo, hi)) for j in range(1, 16)])
+            ops[-1]["beside"] = True
+            swap_ends("aG%d" % r, Gn)
+        else:
+            top = (hi - M) // 16
+            greater(0, 16)
+            greater(96, 112)
+            put = x_lower(Xn, 1536, M, "A", True, "pX0")
+            if left is not None:
+                tt(v("xend"), ve(Xn, 0), ve("gt", 0), ALU.add)
+            names("A", "off", lo // 16, 56)
+            put()
+            send("aX%d" % r, (v("xend"), ve("xland", E)), (ve(Xn, V - E), ve("xland", 0)))
+            recv("aX%d" % r, ve("xland", 0), ve("xland", E))
+            end_results()
+            names("A", "off", 56, 112)
+            dma("S", [(v("yn", lo, M), row(Gn, 0, lo, M))])
+            puts = []
+            for j, (a, b) in enumerate(((16, 32), (32, 64), (64, 80), (80, 96))):
+                diff(a, b)
+                sign(a, b, "V")
+                greater(a, b)
+                a = a if j else 0
+                put = x_lower(Xn, 16 * a, 16 * b, "A" if j < 3 else "V", True, ("pX1", "pX0", "pA", "pL")[j])
+                if j < 2:
+                    put()
+                else:
+                    puts.append(put)
+                if j == 1:
+                    dma("S", [(v("yx", M, M + 1024), v(Xn, M, M + 1024))])
+                    dma("G", [(v("yx", lo, 1024), v("gt", lo, 1024)), (v("yx", 1536, M), v("gt", 1536, M))], True)
+                    wins(1, 32, K, "Y")
+                    wins(2, 0, K, "Y")
+                    wins(3, 0, K, "Y")
+            tt(v("eq", 0, 512), v(Xn, 1024, 1536), v("gt", 1024, 1536), ALU.add)
+            wins(4, 0, K, "Y")
+            wins(5, 0, K, "Y")
+            wins(6, 0, 192, "Y", False, True)
+            from_ends("sinL", "sinR", r * K, True)
+            hm = top - 26
+            puts[0]()
+            puts[1]()
+            names("A", "off2", 0, hm)
+            ts(v("cl"), v("pW", 0, K), 1.0, ALU.min, -1.0, ALU.max)
+            names("V", "off2", hm, hm + 8)
+            tt(v("sf"), v("pS", 0, K), v("cl"), ALU.add)
+            names("V", "off2", hm + 8, top)
+            ends = []
+            if left is not None:
+                ends += [(ve("yn", 0), row("nland", 0, 0, E)), (ve("yx", 0), ve("xland", 0))]
+            if right is not None:
+                ends += [(ve("yn", V - E), row("nland", 0, E, 2 * E)), (ve("yx", V - E), ve("xland", E))]
+            dma("S", ends)
+            dma("S", [(v("yx", 1024, 1536), v("eq", 0, 512))])
+            dma("S", [(v("yx", M + 1024, hi), v(Xn, M + 1024, hi))])
+            dma("S", [(v("ys"), v("sf"))])
+            dma("A", [(v("yn", M, hi), row(Gn, 0, M, hi))])
+    emit(g, T, Q, ops)
+
+
+def emit(g, T, Q, ops):
+    def meets(a, b):
+        for n1, l1, h1 in a:
+            for n2, l2, h2 in b:
+                if n1 == n2 and l1 < h2 and l2 < h1:
+                    return True
+        return False
+
+    for op in ops:
+        op["names"] = set(x[0] for x in op["R"] + op["W"])
+        op["bank"] = set(x for x in op["names"] if SCRATCH.get(x, ("",))[0] == "psum")
+    know = {e: {} for e in Q}
+    pos = {e: 0 for e in Q}
+    nd = 0
+    for k, op in enumerate(ops):
+        e = op["eng"]
+        if op["kind"] == "r":
+            op["tok"], op["clock"], op["waits"] = (op["sem"], 1), {op["sem"]: 1}, []
+            continue
+        waits = []
+        for j in range(k - 1, -1, -1):
+            o = ops[j]
+            if know[e].get(o["tok"][0], 0) >= o["tok"][1] or not (op["names"] & o["names"]):
+                continue
+            if (o["eng"] == "P" and e == "P") or (op.get("beside") and j == k - 1):
+                continue
+            if (meets(op["R"], o["W"]) or meets(op["W"], o["W"]) or meets(op["W"], o["R"])
+                    or (o["eng"] != e and op["bank"] & o["bank"])):
+                waits.append(j)
+                o["seen"] = True
+                for t, x in o["clock"].items():
+                    if know[e].get(t, 0) < x:
+                        know[e][t] = x
+        op["waits"] = waits
+        if op["kind"] == "c":
+            pos[e] += 1
+            op["tok"] = ("e" + e, pos[e])
+        else:
+            op["sem"] = "d%d" % nd
+            nd += 1
+            op["tok"] = (op["sem"], 1)
+        op["clock"] = dict(know[e])
+        op["clock"][op["tok"][0]] = op["tok"][1]
+    count = {e: 0 for e in Q}
+    for op in ops:
+        e = op["eng"]
+        if op["kind"] == "r":
+            continue
+        for j in op["waits"]:
+            o = ops[j]
+            if o["kind"] == "c":
+                Q[e].wait_ge(T.sem[o["tok"][0]], o["val"])
+            else:
+                Q[e].wait_ge(T.sem[o["sem"]], o["n"])
+        if op["kind"] == "c":
+            ins = op["fn"]()
+            if op.get("seen"):
+                count[e] += 1
+                op["val"] = count[e]
+                ins.then_inc(T.sem["e" + e], 1)
+        else:
+            op["fn"](T.sem[op["sem"]])
+    for op in ops:
+        if op["kind"] != "c" and not op.get("seen"):
+            g.wait_ge(T.sem[op["sem"]], op["n"])

@@ -3,46 +3,37 @@ from concourse.mybir import AluOpType, ActivationFunctionType
 
 ALU, AF = AluOpType, ActivationFunctionType
 V, M, E, RO = 3584, 1792, 256, 3
-K = 224
+K, HK = 224, 112
 WID = 4096
 F, B, H, I, U16 = "float32", "bfloat16", "float16", "int32", "uint16"
-SCRATCH = {
-    "hint": ("sbuf", [128, V], I), "G0": ("sbuf", [128, WID], F), "G1": ("sbuf", [128, WID], F),
-    "N0": ("sbuf", [128, WID], F), "N1": ("sbuf", [128, WID], F), "X0": ("sbuf", [128, WID], B), "X1": ("sbuf", [128, WID], B),
-    "val": ("sbuf", [128, V], F), "winV": ("sbuf", [128, WID], F), "winA": ("sbuf", [128, WID], F),
-    "nl": ("sbuf", [128, M], F), "eq": ("sbuf", [128, M], B), "dd": ("sbuf", [128, M], B), "sg": ("sbuf", [128, M], B),
-    "gt": ("sbuf", [128, M], B), "nend": ("sbuf", [128, 2 * E], F), "nland": ("sbuf", [128, 2 * E], F),
-    "xend": ("sbuf", [128, E], B), "xland": ("sbuf", [128, 2 * E], B),
-    "sci": ("sbuf", [128, K], I), "nmi": ("sbuf", [128, K], I), "nmf": ("sbuf", [128, K], F),
-    "s": ("sbuf", [128, K], B), "sf": ("sbuf", [128, K], F), "mk": ("sbuf", [128, 8 * K], B), "q": ("sbuf", [128, 8 * K + 16], B),
-    "t1": ("sbuf", [128, 8 * K], H), "t2": ("sbuf", [128, 8 * K], H), "t3": ("sbuf", [128, 8 * K], B),
-    "bI": ("sbuf", [128, 32], I), "bF": ("sbuf", [128, 16], F), "par": ("sbuf", [128, 128], F),
-    "Ti": ("sbuf", [128, K], I), "Tj": ("sbuf", [128, K], I), "soff": ("sbuf", [128, K], U16),
-    "cV": ("sbuf", [128, 256], F), "cA": ("sbuf", [128, 256], F), "cS": ("sbuf", [128, K], F),
-    "off": ("sbuf", [128, K], U16), "off2": ("sbuf", [128, 112], U16),
-    "evI": ("sbuf", [128, 112], I), "evJ": ("sbuf", [128, 112], I), "Dp": ("sbuf", [128, 112], F), "fl": ("sbuf", [128, 112], F),
-    "pp": ("sbuf", [128, 112], F), "cl": ("sbuf", [128, K], B), "sk": ("sbuf", [128, K], B),
-    "so": ("sbuf", [128, RO * K], B), "soL": ("sbuf", [128, RO * K], B), "soR": ("sbuf", [128, RO * K], B),
-    "sE": ("sbuf", [128, RO * K], B), "sinL": ("sbuf", [128, RO * K], B), "sinR": ("sbuf", [128, RO * K], B),
-    "pidx": ("sbuf", [128, 4], I), "col": ("sbuf", [128, 16], F), "jt": ("sbuf", [128, 128], F), "kio": ("sbuf", [128, 256], F),
-    "rel": ("sbuf", [128, 128], B), "relj": ("sbuf", [128, 144], B), "ab": ("sbuf", [128, 3 * 128], B),
-    "a32": ("sbuf", [128, 144], B), "b32": ("sbuf", [128, 144], B), "sh": ("sbuf", [128, 6 * 128], B), "ta": ("sbuf", [128, 6 * 128], B),
-    "triL": ("sbuf", [128, 128], B), "triU": ("sbuf", [128, 128], B), "half": ("sbuf", [128, 128], B),
-    "ib": ("sbuf", [128, 128], B), "i16": ("sbuf", [128, 128], H), "i896": ("sbuf", [128, 128], B),
-    "i32": ("sbuf", [128, 128], F), "ineg": ("sbuf", [128, 128], B), "band": ("sbuf", [128, 4 * 128], F),
-    "Z": ("sbuf", [128, 144], B), "U": ("sbuf", [128, 144], B), "Yu": ("sbuf", [128, 144], B), "Yl": ("sbuf", [128, 144], B),
-    "Y": ("sbuf", [128, 144], B), "tau": ("sbuf", [128, K], H), "uu": ("sbuf", [128, 112], H), "keep": ("sbuf", [128, K], B),
-    "kt": ("sbuf", [128, K], F), "ones": ("sbuf", [128, K], B), "cst": ("sbuf", [128, 96], B), "zero": ("sbuf", [128, 256], F),
-    "pS": ("psum", [128, 512], F), "pT": ("psum", [128, 512], F), "pA": ("psum", [128, 512], F), "pL": ("psum", [128, 512], F),
-    "pO": ("psum", [128, 512], F), "pW": ("psum", [128, 512], F), "pX0": ("psum", [128, 512], F), "pX1": ("psum", [128, 512], F),
-}
-NDMA = 100
+SCRATCH = {}
+for _n, _d, _names in (
+        (V, I, "hint"), (V, F, "val"), (V, B, "gs"), (WID, B, "X0 X1"), (WID, F, "winV winA G0 G1 N0 N1"), (M, F, "nl"),
+        (M, B, "eq xo"), (2 * E, F, "nland"), (4 * E, F, "pland"), (2 * E, B, "xland"),
+        (K, I, "sci nmi Ti Tj"), (K, F, "nmf sf tI"), (K, B, "s0 s1 s2 cl so sE sinL sinR"),
+        (8 * K, B, "mk mo"), (8 * K + 16, B, "q"), (8 * K, H, "t1 t2"), (4 * K, B, "t3"), (9 * HK, H, "te"),
+        (K, H, "pz fz"), (32, I, "bI"), (128, F, "par cU cL pp jt i32 bp bn"), (K, U16, "soff"), (256, F, "cV cA kio zero"),
+        (128, U16, "oU oL o2"), (HK, I, "evI evJ"), (HK, F, "Dp fl"), (32, B, "sx"), (4, I, "pidx"), (16, F, "col"),
+        (128, B, "rel triL triU half blk1 triB ib i896 ineg hb"), (144, B, "relj a32 b32 Z U Y"), (3 * 128, B, "ab"),
+        (256, B, "dk dn"), (4 * 128, B, "sh"), (128, H, "h16 i16"), (4 * 128, F, "band"), (HK, H, "uu"), (48, B, "cst")):
+    for _x in _names.split():
+        SCRATCH[_x] = ("sbuf", [128, _n], _d)
+for _k in range(8):
+    SCRATCH["B%d" % _k] = ("psum", [128, 512], F)
+NDMA = 110
 SEMAPHORES = (["eV", "eA", "eP", "eG"] + ["d%d" % i for i in range(NDMA)]
-              + ["%s%d" % (k, r) for k in ("aS", "aO", "aN", "aM", "aG", "aX") for r in range(RO)])
-KA = (146, 114, 118)
-SHIFTS = (14, 15, -14, -15, -1, 1)
-QUARTERS = ((1536, M), (0, 512), (512, 1024), (1024, 1536))
+              + ["%s%d" % (k, r) for k in ("aS", "aX") for r in range(RO)]
+              + ["%s%d" % (k, r) for k in ("aG", "aP") for r in range(RO - 1)] + ["aN"])
+KA = (146, 114, 114)
+KG = 160
+NS = 68
+SHIFTS = (14, 15, -14, -15)
 BIG = 1 << 20
+CYC, PEC, GATH, SCAT, WAKE, RATE = 0.00083, 0.6, 1.25, 2.2, 0.13, 4.0e5
+AHEAD, SLACK, DEPTH = {"V": 72, "A": 40, "P": 160}, 0.04, 24
+ROT = 18
+PE_, PM1, PM2 = (2, 34), (34, 72), (72, 114)
+CP = ((0, 18), (18, 36), (36, 56), (56, 74), (74, 94), (94, HK))
 
 
 def rank_program(g, core, T, topo):
@@ -52,25 +43,24 @@ def rank_program(g, core, T, topo):
     nr = len(T.cores)
     left = T.cores[rank - 1] if rank > 0 else None
     right = T.cores[rank + 1] if rank + 1 < nr else None
+    hasl, hasr = left is not None, right is not None
+    lo = E if hasl else 0
+    hi = V - E if hasr else V
+    wid = V + E * (hasl + hasr)
 
-    def ext_first(r):
-        return V
+    def ext_last(k):
+        return V + (E if k > 0 else 0)
 
-    def ext_last(r):
-        return V + (E if r > 0 else 0)
-
-    wid = V + (E if left is not None else 0) + (E if right is not None else 0)
-    lo = E if left is not None else 0
-    hi = V - E if right is not None else V
     Q = {"V": g.vector, "A": g.scalar, "P": g.tensor, "S": g.sync, "G": g}
     ops = []
+    lag = [0]
 
     def v(name, a=None, b=None, st=None):
         if a is None:
-            return (T[name][:], [(name, 0, BIG)])
+            return (T[name][:], [(name, 0, BIG, None)], int(T[name].shape[1]))
         if st is None:
-            return (T[name][:, a:b], [(name, a, b)])
-        return (T[name][:, a:b:st], [(name, a, b)])
+            return (T[name][:, a:b], [(name, a, b, None)], b - a)
+        return (T[name][:, a:b:st], [(name, a, b, None)], len(range(a, b, st)))
 
     def ve(name, a):
         return v(name, a, a + E)
@@ -81,14 +71,14 @@ def rank_program(g, core, T, topo):
     def w(name, o):
         return v(name, o, o + 128)
 
-    def shift(s, name="sh"):
-        return w(name, 128 * SHIFTS.index(s))
+    def shift(s):
+        return w("sh", 128 * SHIFTS.index(s))
 
     def row(name, r, a, b):
-        return (T[name][r::16, a:b], [(name, a, b)])
+        return (T[name][r::16, a:b], [(name, a, b, r)], (b - a) // 16)
 
-    def ind(name, n, offs, a, b):
-        return (T[name][:, 0:n].indirect(T[offs][:, a:b]), [(name, 0, n), (offs, a, b)])
+    def ind(name, offs, a, b, n):
+        return (T[name][:, 0:n].indirect(T[offs][:, a:b]), [(name, 0, n, None), (offs, a, b, None)], 16 * (b - a))
 
     def blk(name, b, o=0, n=1):
         return v(name, o + b * K, o + (b + n) * K)
@@ -103,33 +93,50 @@ def rank_program(g, core, T, topo):
                 out += x[1]
         return out
 
-    def add(eng, kind, fn, R, W, n=1, sem=None):
-        ops.append({"eng": eng, "kind": kind, "fn": fn, "R": R, "W": W, "n": n, "sem": sem})
+    def add(eng, kind, fn, R, W, n=1, sem=None, cost=0.0):
+        ops.append({"eng": eng, "kind": kind, "fn": fn, "R": R, "W": W, "n": n, "sem": sem, "cost": cost, "key": len(ops) + lag[0]})
+
+    def wide(x):
+        return SCRATCH[x[1][0][0]][2] in (F, I) if x[1][0][0] in SCRATCH else x[1][0][0] not in ("x", "yx")
+
+    def cyc(out, *ins, both=False, fix=0.0):
+        if len(out[1]) > 1:
+            return 0.06 + CYC * SCAT * out[2]
+        if ins and len(ins[0][1]) > 1:
+            return 0.06 + CYC * GATH * out[2]
+        k = 1.0 if fix or any(wide(x) for x in (out,) + ins) else 0.5
+        if both and not any(SCRATCH[x[1][0][0]][0] == "psum" for x in ins):
+            k *= 2
+        return (fix or 0.05) + CYC * max(64, k * out[2])
 
     def ts(out, in0, s1, op0, s2=None, op1=None):
         if op1 is None:
-            add("V", "c", lambda: g.vector.tensor_scalar(out[0], in0[0], ap(s1), None, op0), regs(in0, s1), out[1])
+            add("V", "c", lambda: g.vector.tensor_scalar(out[0], in0[0], ap(s1), None, op0), regs(in0, s1), out[1],
+                cost=cyc(out, in0))
         else:
-            add("V", "c", lambda: g.vector.tensor_scalar(out[0], in0[0], ap(s1), ap(s2), op0, op1), regs(in0, s1, s2), out[1])
+            add("V", "c", lambda: g.vector.tensor_scalar(out[0], in0[0], ap(s1), ap(s2), op0, op1), regs(in0, s1, s2), out[1],
+                cost=cyc(out, in0))
 
     def tt(out, a, b, op):
-        add("V", "c", lambda: g.vector.tensor_tensor(out[0], a[0], b[0], op), regs(a, b), out[1])
+        add("V", "c", lambda: g.vector.tensor_tensor(out[0], a[0], b[0], op), regs(a, b), out[1], cost=cyc(out, a, b, both=True))
 
     def cp(out, a):
-        add("V", "c", lambda: g.vector.tensor_copy(out[0], a[0]), regs(a) + out[1][1:], out[1][:1])
+        add("V", "c", lambda: g.vector.tensor_copy(out[0], a[0]), regs(a) + out[1][1:], out[1][:1], cost=cyc(out, a))
 
     def ms(out, x):
-        add("V", "c", lambda: g.vector.memset(out[0], x), [], out[1])
+        add("V", "c", lambda: g.vector.memset(out[0], x), [], out[1], cost=cyc(out))
 
-    def scan(out, a):
-        add("V", "c", lambda: g.vector.tensor_tensor_scan(out[0], a[0], a[0], 0.0, ALU.add, ALU.max), a[1], out[1])
+    def scan(out, a, init=0.0):
+        add("V", "c", lambda: g.vector.tensor_tensor_scan(out[0], a[0], a[0], ap(init), ALU.add, ALU.max), regs(a, init), out[1],
+            cost=cyc(out, a))
 
     def act(out, a, func, bias=0.0, scale=1.0):
         if bias == 0.0 and scale == 1.0:
-            add("A", "c", lambda: g.scalar.activation(out[0], a[0], func), regs(a) + out[1][1:], out[1][:1])
+            add("A", "c", lambda: g.scalar.activation(out[0], a[0], func), regs(a) + out[1][1:], out[1][:1],
+                cost=cyc(out, a, fix=0.06))
         else:
             add("A", "c", lambda: g.scalar.activation(out[0], a[0], func, bias=ap(bias), scale=ap(scale)),
-                regs(a, bias, scale) + out[1][1:], out[1][:1])
+                regs(a, bias, scale) + out[1][1:], out[1][:1], cost=cyc(out, a, fix=0.06) + (1.3 if func == AF.Silu else 0.0))
 
     def gat(eng, out, a):
         if eng == "V":
@@ -138,26 +145,31 @@ def rank_program(g, core, T, topo):
             act(out, a, AF.Identity)
 
     def mm(out, l, r, start=False, stop=False):
-        add("P", "c", lambda: g.tensor.matmul(out[0], l[0], r[0], start, stop), regs(l, r), out[1])
+        add("P", "c", lambda: g.tensor.matmul(out[0], l[0], r[0], start, stop), regs(l, r), out[1],
+            cost=0.015 + CYC * PEC * max(64, r[2]) * (4 if wide(l) else 1))
 
     def iota(out, pat, base, cm, flag=True):
         if flag:
-            add("G", "c", lambda: g.iota(out[0], pat, base, cm, allow_small_or_imprecise_dtypes=True), [], out[1])
+            add("G", "c", lambda: g.iota(out[0], pat, base, cm, allow_small_or_imprecise_dtypes=True), [], out[1],
+                cost=0.13 + 2 * CYC * out[2])
         else:
-            add("G", "c", lambda: g.iota(out[0], pat, base, cm), [], out[1])
+            add("G", "c", lambda: g.iota(out[0], pat, base, cm), [], out[1], cost=0.13)
 
-    def dma(eng, pairs, accum=False):
+    def pick(out, a, op, fill, base, pat=((1, 128),), cm=-1):
+        add("G", "c", lambda: g.affine_select(out[0], a[0], [list(x) for x in pat], op, fill, base, cm), a[1], out[1],
+            cost=0.17 + 2 * CYC * out[2])
+
+    def dma(eng, pairs):
         def fn(sem):
             for o, i in pairs:
-                if accum:
-                    g.dma_start(o[0], i[0], accum_op=ALU.add).then_inc(sem, 16)
-                else:
-                    Q[eng].dma_start(o[0], i[0]).then_inc(sem, 16)
-        R, W = [], []
+                Q[eng].dma_start(o[0], i[0]).then_inc(sem, 16)
+        R, W, nb = [], [], 0
         for o, i in pairs:
             R += i[1]
             W += o[1]
-        add(eng, "d", fn, R, W, 16 * len(pairs))
+            x = o if o[1][0][0] in SCRATCH else i
+            nb += 128 * x[2] * (4 if wide(x) else 2)
+        add(eng, "d", fn, R, W, 16 * len(pairs), cost=(0.06 * len(pairs), 1.5, nb / RATE))
 
     def half_mask(src, dst):
         en = topo.engines(src, dst)
@@ -165,418 +177,559 @@ def rank_program(g, core, T, topo):
         part = en[h:] if T.rank_of(dst) > T.rank_of(src) else en[:h]
         return sum(1 << e for e in part), len(part)
 
-    def send(sem, to_left, to_right):
-        tr, R, cnt = [], [], 0
-        for dst, x in ((left, to_left), (right, to_right)):
-            if dst is None or x is None:
+    def swap(sem, first, last, land_first, land_last, at_left=None):
+        tr, R, W, cnt, got = [], [], [], 0, 0
+        for other, src, there, here in ((left, first, at_left or land_last, land_first), (right, last, land_first, land_last)):
+            if other is None:
                 continue
-            rid, pid, _se = topo.addr(dst)
-            mask, k = half_mask(core, dst)
+            rid, pid, _se = topo.addr(other)
+            mask, k = half_mask(core, other)
             tr.append(RemoteDMATransfer(dst_ids=[DstId(rid=rid, pnc=pid)], dma_engine_mask=mask, remote_sem=T.sem[sem],
-                                        src=x[0][0], dst=x[1][0]))
-            R += x[0][1]
+                                        src=src[0], dst=there[0]))
+            R += src[1]
+            W += here[1]
             cnt += k
-        if tr:
-            add("G", "d", lambda s: g.remote_dma_fused(tr, local_sem=s), R, [], cnt)
+            got += half_mask(other, core)[1]
+        nb = len(tr) * 128 * first[2] * (4 if wide(first) else 2)
+        add("G", "d", lambda s: g.remote_dma_fused(tr, local_sem=s), R, [], cnt, cost=(0.4, 1.6, nb / RATE))
+        ops[-1]["pair"] = sem
+        add(None, "r", None, [], W, got, sem)
 
-    def recv(sem, from_left, from_right):
-        W, cnt = [], 0
-        for src, x in ((left, from_left), (right, from_right)):
-            if src is None or x is None:
-                continue
-            W += x[1]
-            cnt += half_mask(src, core)[1]
-        if cnt:
-            add(None, "r", None, [], W, cnt, sem)
-
-    def swap_ends(sem, name):
-        send(sem, (ve(name, 0), ve(name, ext_last(rank - 1))), (ve(name, V - E), ve(name, ext_first(rank + 1))))
-        recv(sem, ve(name, ext_first(rank)), ve(name, ext_last(rank)))
-
-    def both(sem, src, at_left, at_right):
-        send(sem, (src, at_right), (src, at_left))
-        recv(sem, at_left, at_right)
-
-    IB = v("ib")
+    IB, I16 = v("ib"), v("i16")
     dma("S", [(v("sci"), v("sc"))])
     dma("S", [(v("nmi"), v("nm"))])
     iota(c("pidx", 0), [[0, 1]], 0, 1, False)
     iota(v("jt"), [[64, 8], [1, 16]], 0, 0)
+    iota(v("cst"), [[1792, 3], [0, 16]], -1792, 0)
+    iota(v("q", 0, 16), [[0, 16]], 0, 0)
+    ka = KA[0]
+    iota(v("val", 0, 16 * (K - KG)), [[1, K - KG], [K, 16]], 64, 0)
+    iota(v("val", 16 * (K - KG), 16 * ka), [[1, ka - K + KG], [K, 16]], 64 + K - KG, 0)
+    iota(v("val", 16 * ka, 16 * KG), [[1, KG - ka], [K, 16]], 64 + ka, 0)
     iota(v("kio"), [[1, 256]], 0, 0)
-    iota(v("val", 0, 16 * KA[0]), [[1, KA[0]], [K, 16]], 64, 0)
-    iota(v("val", 16 * KA[0], V), [[1, K - KA[0]], [K, 16]], 64 + KA[0], 0)
+    iota(v("tI"), [[1, 2], [32, HK]], 0, 2)
     ms(v("zero"), 0.0)
     dma("S", [(row("winA", 0, 0, WID), v("zero")), (row("winV", 0, 0, WID), v("zero"))])
     dma("S", [(v("hint", 0, M), v("hi", 0, M))])
     ts(c("pidx", 1), c("pidx", 0), 15, ALU.bitwise_and)
     ts(c("pidx", 2), c("pidx", 0), 4, ALU.logical_shift_right)
-    ms(v("cst", 0, 16), -1792.0)
     cp(c("col", 0), c("pidx", 1))
     ts(c("col", 1), c("pidx", 2), -64.0, ALU.mult)
-    ms(v("cst", 16, 48), -0.25)
     tt(c("col", 2), c("col", 0), c("col", 1), ALU.subtract)
-    ms(v("cst", 48, 64), -1.0)
     ts(v("rel"), v("jt"), c("col", 2), ALU.subtract)
-    ms(v("cst", 64, 80), 0.0)
-    ms(v("cst", 80, 96), 1792.0)
-    ms(v("q", 0, 16), 0.0)
     for j, bias in enumerate((0.0, -8.0, 8.0)):
         act(w("ab", 128 * j), v("rel"), AF.Abs, bias=bias)
     ts(IB, v("rel"), 0.0, ALU.is_equal)
-    ts(v("i16"), v("rel"), 0.0, ALU.is_equal)
+    act(v("i896"), IB, AF.Silu, scale=896.0)
+    act(v("val", 16 * KG, V), v("val", 0, 16 * (K - KG)), AF.Identity, bias=float(KG))
+    ts(I16, v("rel"), 0.0, ALU.is_equal)
     ts(v("half"), w("ab", 0), 15.5, ALU.is_lt, 0.5, ALU.mult)
     ts(v("triL"), w("ab", 128), 7.5, ALU.is_lt)
     ts(v("triU"), w("ab", 256), 7.5, ALU.is_lt)
-    cp(v("s"), v("sci"))
-    act(v("i896"), IB, AF.Silu, scale=896.0)
-    act(c("col", 9), c("col", 1), AF.Identity, bias=-16.0, scale=0.25)
-    act(c("col", 7), c("col", 0), AF.Identity, bias=-(lo + hi - 1) / 2.0, scale=224.0)
-    act(c("col", 8), c("col", 0), AF.Sign, bias=-7.5)
-    act(c("col", 4), c("col", 0), AF.Identity, bias=-896.0 - 895.75, scale=224.0)
-    act(c("col", 6), c("col", 0), AF.Identity, bias=1.0)
-    act(v("relj"), v("kio", 0, 144), AF.Identity, bias=c("col", 9))
-    act(c("col", 5), c("col", 8), AF.Identity, bias=c("col", 4), scale=-895.75)
-    act(v("a32"), v("relj"), AF.Abs, bias=0.5)
-    act(v("b32"), v("relj"), AF.Abs)
-    act(v("Z"), v("a32"), AF.Relu, bias=1.5, scale=-1.0)
-    act(v("U"), v("b32"), AF.Relu, bias=1.0, scale=-1.0)
-    act(v("a32"), v("relj"), AF.Abs, bias=-8.0)
-    act(v("Yu"), v("U"), AF.Identity, scale=-1.0)
-    act(v("Yl"), v("a32"), AF.Relu, bias=1.0, scale=-1.0)
+    cp(v("s0"), v("sci"))
 
-    def more_constants(step):
-        if step == 0:
-            for s in SHIFTS:
-                act(shift(s, "ta"), v("rel"), AF.Abs, bias=float(-s))
-            act(v("sh"), v("ta"), AF.Relu, bias=1.0, scale=-1.0)
-        else:
-            act(v("kt"), v("kio", 0, K), AF.Abs, bias=c("col", 7))
-            act(v("ones"), v("kio", 0, K), AF.Identity, bias=1.0, scale=0.0)
-            act(v("kt"), v("kt"), AF.Sign, bias=(hi - lo) / 2.0, scale=-1.0)
-            act(v("i32"), IB, AF.Identity)
-            act(v("keep"), v("kt"), AF.Relu)
-            act(w("band", 128), shift(15), AF.Identity)
-            act(w("band", 384), shift(-15), AF.Identity, scale=-1.0)
-            act(v("ineg"), IB, AF.Identity, scale=-1.0)
-            for a in ([0] if left is not None else []) + ([V - E] if right is not None else []):
-                act(ve("N1", a), v("zero"), AF.Identity)
-
-    def x_lower(X, a, b, eng, with_gt, bank):
-        px = v(bank, 0, b - a)
-        mm(px, IB, v(X, a, b), True)
-        mm(px, IB, v("dd", a, b))
-        if with_gt:
-            mm(px, IB, v("gt", a, b))
-        mm(px, v("ineg"), v("sg", a, b), False, True)
-        return lambda: gat(eng, v(X, M + a, M + b), px)
-
-    def from_ends(at_left, at_right, o, stop):
-        arr = []
-        if right is not None:
-            arr += [(192, K, 14, v(at_right, o, o + 32)), (0, 192, 15, v(at_right, o + 32, o + K))]
-        if left is not None:
-            arr += [(0, 32, -14, v(at_left, o + 192, o + K)), (32, K, -15, v(at_left, o, o + 192))]
-        for j, (a, b, s, src) in enumerate(arr):
-            mm(v("pS", a, b), shift(s), src, False, stop and j == len(arr) - 1)
-
-    for r in range(RO):
-        C = 4 + 2 * r
-        n = V if r == 0 else wid
-        Gc, Nc, Xc = "G%d" % (r % 2), "N%d" % (r % 2), "X%d" % (r % 2)
-        Gn, Nn, Xn = "G%d" % (1 - r % 2), "N%d" % (1 - r % 2), "X%d" % (1 - r % 2)
-        last = r == RO - 1
-        ka = KA[r]
-        mm(v("pS", 0, 48), IB, v("cst", 0, 48), True)
-        mm(v("pS", 0, 48), IB, v("cst", 48, 96))
-        uppers = []
-        if r > 0:
-            for (a, b), bank in zip(QUARTERS, ("pX0", "pX1", "pA", "pL")):
-                mm(v(bank, 0, b - a), IB, v(Xc, a, b), True)
-                mm(v(bank, 0, b - a), IB, v("gt", a, b), False, True)
-                uppers.append(lambda o=v(Xc, a, b), i=v(bank, 0, b - a): gat("A", o, i))
-        for b in range(C):
-            ts(blk("mk", b), v("s"), float(C - 1 - b), ALU.is_equal)
-        scan(v("q", 16, 16 + C * K), v("mk", 0, C * K))
+    def counts(C, stop):
         e_all = v("q", 15, 16 + C * K, K)
-        mm(v("pS", 16, 17 + C), v("half"), e_all)
-        mm(v("pS", 32, 33 + C), v("half"), e_all)
-        mm(v("pS", 0, C), v("triL"), v("q", 15 + K, 16 + C * K, K))
-        mm(v("pS", 0, C), v("triU"), v("q", 15, 16 + (C - 1) * K, K), False, True)
+        mm(v("B7", 16, 17 + C), v("half"), e_all)
+        mm(v("B7", 32, 33 + C), v("half"), e_all, False, stop)
 
-        def member(b, m=1):
+    def window_columns(bank, const, ka):
+        for a, b in ((0, ka), (ka, K)):
+            ts(v("Ti", a, b), v(bank, a, b), const, ALU.add, 4097.0, ALU.mult)
+            ts(v("Tj", a, b), v("Ti", a, b), 4, ALU.logical_shift_right, 4095, ALU.bitwise_and)
+            cp(v("soff", a, b), v("Tj", a, b))
+
+    def sort_blocks(C):
+        pT = v("B5", 0, K)
+        mm(v("B7", 0, 48), IB, v("cst"), True)
+        for b in range(C):
+            ts(blk("mk", b), v("s0"), float(C - 1 - b), ALU.is_equal)
+        scan(v("q", 16, 16 + C * K), v("mk", 0, C * K))
+        cp(v("nmf"), v("nmi"))
+        dma("S", [(row("N0", 0, 0, V), v("nmf"))])
+        dma("S", [(v("hint", M, V), v("hi", M, V))])
+        dma("S", [(row("N0", j, 0, V), row("N0", 0, 0, V)) for j in range(1, 16)])
+        counts(C, False)
+        mm(v("B7", 0, C), v("triL"), v("q", 15 + K, 16 + C * K, K))
+        mm(v("B7", 0, C), v("triU"), v("q", 15, 16 + (C - 1) * K, K), False, True)
+
+        def member(b, m):
             tt(blk("t3", b, 0, m), blk("mk", b, 0, m), blk("q", b, 16, m), ALU.mult)
             for j in range(b, b + m):
-                mm(v("pT", 0, K), IB, blk("t3", j), j == 0)
+                mm(pT, IB, blk("t3", j), j == 0)
 
         def base(b):
             ts(blk("t1", b), blk("mk", b), c("par", b), ALU.mult)
-            mm(v("pT", 0, K), v("i16"), blk("t1", b))
+            mm(pT, I16, blk("t1", b))
 
-        def floats(b):
-            act(blk("q", b, 16), blk("t3", b), AF.Sign, bias=c("par", 80 + b), scale=-1.0)
-            mm(v("pT", 0, K), v("i896"), blk("q", b, 16))
-
-        if r == 0:
-            cp(v("nmf"), v("nmi"))
-            dma("S", [(row("N0", 0, 0, V), v("nmf"))])
-            dma("S", [(v("hint", M, V), v("hi", M, V))])
-            dma("S", [(row("N0", j, 0, V), row("N0", 0, 0, V)) for j in range(1, 16)])
         member(0, 2)
-        cp(v("bI"), v("pS", 16, 48))
-        member(2)
-        tt(v("par", 0, C), v("pS", 0, C), v("bI", 0, C), ALU.subtract)
+        ts(v("bI"), v("B7", 16, 48), -0.25, ALU.add)
+        member(2, 1)
+        tt(v("par", 0, C), v("B7", 0, C), v("bI", 0, C), ALU.subtract)
         tt(v("par", 16, 16 + C), v("bI", 16, 16 + C), v("bI", 1, 1 + C), ALU.subtract)
         tt(v("par", 32, 32 + C), v("bI", 1, 1 + C), v("par", 0, C), ALU.subtract)
         base(0)
         tt(v("par", 64, 64 + C), v("par", 32, 32 + C), v("par", 16, 16 + C), ALU.subtract)
-        ts(v("par", 48, 48 + C), v("par", 32, 32 + C), -1792.5, ALU.add, 0.5, ALU.max)
-        ts(v("par", 80, 80 + C), v("par", 64, 64 + C), -0.5, ALU.add, 0.5, ALU.max)
-        base(1)
-        for b in range(3, C):
-            member(b)
-            base(b - 1)
-            floats(b - 3)
-        base(C - 1)
-        floats(C - 3)
-        floats(C - 2)
+        ts(v("par", 48, 48 + C), v("par", 32, 32 + C), -1791.5, ALU.add, 0.5, ALU.max)
+        ts(v("par", 80, 80 + C), v("par", 64, 64 + C), 0.5, ALU.add, 0.5, ALU.max)
+        member(3, 1)
+        for b in range(C - 1):
+            act(blk("mo", b), blk("t3", b), AF.Sign, bias=c("par", 80 + b), scale=-1.0)
+        for b in range(1, C):
+            base(b)
         for b in range(C):
             ts(blk("t2", b), blk("t3", b), c("par", 48 + b), ALU.is_gt, c("par", 16 + b), ALU.mult)
+            mm(pT, I16, blk("t2", b))
+        for b in range(C - 1):
+            mm(pT, v("i896"), blk("mo", b), False, b == C - 2)
+        window_columns("B5", float(1791 - 896 * (C - 1)), KA[0])
+
+    def sort_lists(C, s, ka):
+        hc = C // 2
+        mm(v("B7", 16, 48), v("ineg"), v("cst", 16, 48), True)
+        for k in range(hc):
+            for b in (2 * k, 2 * k + 1):
+                ts(blk("mk", b), v(s), float(C - 1 - b), ALU.is_equal)
+            scan(blk("q", 2 * k, 16, 2), blk("mk", 2 * k, 0, 2), c("q", 15 + 2 * k * K))
+        counts(C, True)
+        for j in range(hc):
+            mm(v("B%d" % j, 0, 2 * K), v("blk1"), blk("q", 2 * j, 15, 2), True)
+            mm(v("B%d" % j, 0, 2 * K), v("triB"), blk("mk", 2 * j, 0, 2), False, True)
+        for j in range(hc):
+            ts(blk("t1", 2 * j, 0, 2), v("B%d" % j, 0, 2 * K), -5888.0, ALU.add, -2048.0, ALU.max)
+            if j == hc - 3:
+                ts(v("bI"), v("B7", 16, 48), -0.25, ALU.add)
+            if j == hc - 2:
+                tt(v("par", 16, 16 + C), v("bI", 0, C), v("bI", 1, 1 + C), ALU.subtract)
+                tt(v("par", 32, 32 + C), v("bI", 16, 16 + C), v("bI", 1, 1 + C), ALU.add)
+            for b in (2 * j, 2 * j + 1):
+                mm(v("B4", 0, K), I16, blk("t1", b), b == 0, b == C - 1)
+        ts(v("pz"), v("B4", 0, K), 2048.0 * (C - 1), ALU.add)
+        mm(v("B5", 0, K), v("h16"), v("pz"), True)
         for b in range(C):
-            mm(v("pT", 0, K), v("i16"), blk("t2", b), False, b == C - 1)
-        for put in uppers:
-            put()
-        ts(v("par", 96, 97 + C), v("pS", 16, 17 + C), -896.0, ALU.add)
-        cp(v("bF"), v("bI", 0, 16))
+            ts(blk("t2", b), v("pz"), c("par", 32 + b), ALU.is_ge, c("par", 16 + b), ALU.mult)
+            mm(v("B5", 0, K), I16, blk("t2", b), False, b == C - 1)
+        ts(v("fz"), v("B5", 0, K), -896.25, ALU.is_lt, 1792.0, ALU.mult)
+        mm(v("B0", 0, K), I16, v("pz"), True)
+        for b in range(C):
+            mm(v("B0", 0, K), I16, blk("t2", b))
+        mm(v("B0", 0, K), I16, v("fz"), False, True)
+        window_columns("B0", 1792.0, ka)
+
+    def x_low(X, px, a, b):
+        mm(px, IB, v(X, a, b), True)
+        mm(px, IB, v(X, M + a, M + b))
+        mm(px, IB, v("gs", a, b))
+        mm(px, v("ineg"), v("gs", M + a, M + b), False, True)
+
+    def x_up(X, a, b):
+        tt(v(X, a, b), v(X, a, b), v("gs", a, b), ALU.add)
+
+    def from_ends(at_left, at_right):
+        arr = []
+        if hasr:
+            arr += [(192, K, 14, v(at_right, 0, 32)), (0, 192, 15, v(at_right, 32, K))]
+        if hasl:
+            arr += [(0, 32, -14, v(at_left, 192, K)), (32, K, -15, v(at_left, 0, 192))]
+        for j, (a, b, s, src) in enumerate(arr):
+            mm(v("B1", a, b), shift(s), src, False, j == len(arr) - 1)
+
+    for r in range(RO):
+        C = 4 + 2 * r
+        Gc, Nc, Xc = "G%d" % (r % 2), "N%d" % (r % 2), "X%d" % (r % 2)
+        Gn, Nn, Xn = "G%d" % (1 - r % 2), "N%d" % (1 - r % 2), "X%d" % (1 - r % 2)
+        last = r == RO - 1
+        ka = KA[r]
+        rho = 15 - r
+        pl = 2 * E * r
+        n = V if r == 0 else wid
         if r == 0:
-            more_constants(0)
-        ts(v("Ti"), v("pT", 0, K), float(1792 - 896 * (C - 1)), ALU.add, 4097.0, ALU.mult)
-        for a, b in ((0, ka), (ka, K)):
-            ts(v("Tj", a, b), v("Ti", a, b), 4, ALU.logical_shift_right, 4095, ALU.bitwise_and)
-        for a, b in ((0, ka), (ka, K)):
-            cp(v("soff", a, b), v("Tj", a, b))
-        act(ind("winA", WID, "soff", 0, ka), v("val", 0, 16 * ka), AF.Silu)
+            sort_blocks(C)
+        else:
+            sort_lists(C, "s%d" % r, ka)
+        act(ind("winA", "soff", 0, ka, WID), v("val", 0, 16 * ka), AF.Silu)
         dma("A", [(v("cA"), row("winA", 0, 0, WID))])
-        cp(ind("winV", WID, "soff", ka, K), v("val", 16 * ka, V))
+        cp(ind("winV", "soff", ka, K, WID), v("val", 16 * ka, V))
         dma("S", [(v("cV"), row("winV", 0, 0, WID))])
         if r == 0:
             dma("A", [(v("X0", 0, V), v("x"))])
-            more_constants(1)
-            ts(v("tau"), v("kio", 0, K), c("col", 5), ALU.add)
-            ts(v("uu"), v("kio", 0, 112), 16.0, ALU.mult, c("col", 6), ALU.add)
-            tt(v("Y"), v("Yu"), v("Yl"), ALU.add)
-            tt(w("band", 0), shift(-1), IB, ALU.subtract)
-            tt(w("band", 256), IB, shift(1), ALU.subtract)
+            act(v("bp"), v("half"), AF.Identity, scale=2.0)
+            act(v("bn"), v("half"), AF.Identity, scale=-2.0)
+            act(v("blk1"), v("half"), AF.Identity, scale=2.0)
+            pick(w("band", 128), v("bp"), ALU.is_equal, 0.0, -15)
+            pick(w("band", 384), v("bn"), ALU.is_equal, 0.0, 15)
+            pick(v("bp"), v("bp"), ALU.is_equal, 0.0, 1)
+            pick(v("bn"), v("bn"), ALU.is_equal, 0.0, -1)
+            pick(w("band", 0), v("bp"), ALU.not_equal, -1.0, 0)
+            pick(w("band", 256), v("bn"), ALU.not_equal, 1.0, 0)
+            pick(v("triB"), v("triL"), ALU.not_equal, 4096.0, 0)
+            inner = ((0, 8), (1, 16))
+            pick(w("dk", 0), IB, ALU.not_equal, 0.0, 0 if hasl else 99, inner, 0)
+            pick(w("dk", 128), w("dk", 0), ALU.not_equal, 0.0, -15 if hasr else 99, inner, 0)
+            act(v("ineg"), IB, AF.Identity, scale=-1.0)
+            pick(w("dn", 0), v("ineg"), ALU.is_equal, 0.0, -1, inner, 0)
+            pick(w("dn", 128), v("ineg"), ALU.is_equal, 0.0, -14, inner, 0)
+            for a, b, at in ((M + 1536, V, ext_last(rank) if hasr else M), (16 * ka, M + 1536, 16 * ka + E), (M, 16 * ka, M + E),
+                             (1536, M, 0), (E, 1536, 2 * E), (0, E, V if hasl else E)):
+                iota(v("val", a, b), [[1, b - a]], 64 + at, 0)
             cp(v("G0", 0, V), v("hint"))
-            if left is not None:
-                iota(v("val", 0, V, 16), [[1, K]], 64 + ext_first(rank), 0)
-                iota(v("val", 1, 16 * 32, 16), [[1, 32]], 64 + ext_first(rank) + K, 0)
-            if right is not None:
-                iota(v("val", 16 * 192 + 14, V, 16), [[1, 32]], 64 + ext_last(rank), 0)
-                iota(v("val", 15, V, 16), [[1, K]], 64 + ext_last(rank) + 32, 0)
+            dma("S", [(row(Gc, rho, 0, V), row(Nc, 0, 0, V))])
+            act(c("col", 9), c("col", 1), AF.Identity, bias=-16.0, scale=0.25)
+            act(c("col", 3), c("col", 1), AF.Identity, bias=-895.0, scale=0.25)
+            act(c("col", 8), c("col", 0), AF.Sign, bias=-7.5)
+            act(c("col", 4), c("col", 0), AF.Identity, bias=895.5, scale=-224.0)
+            act(c("col", 11), c("col", 8), AF.Identity, bias=c("col", 4), scale=895.75)
+            act(c("col", 10), c("col", 1), AF.Identity, bias=-0.25, scale=-0.25)
+            act(v("relj"), v("kio", 0, 144), AF.Identity, bias=c("col", 9))
+            act(v("a32"), v("relj"), AF.Abs, bias=0.5)
+            act(v("b32"), v("relj"), AF.Abs)
+            act(v("i32"), IB, AF.Identity)
+            act(v("hb"), IB, AF.Identity, scale=0.5)
+            act(v("Z"), v("a32"), AF.Relu, bias=1.5, scale=-1.0)
+            act(v("U"), v("b32"), AF.Relu, bias=1.0, scale=-1.0)
+            ts(v("uu", 0, ROT), v("tI", K - ROT, K), 0.5, ALU.mult, c("col", 3), ALU.add)
+            ts(v("uu", ROT, HK), v("tI", HK, K - ROT), 0.5, ALU.mult, c("col", 3), ALU.add)
         else:
-            puts = [x_lower(Xc, a, b, "A", False, bank) for (a, b), bank in zip(QUARTERS, ("pX0", "pX1", "pW", "pL"))]
-            puts[0]()
-            swap_ends("aX%d" % (r - 1), Xc)
-            for put in puts[1:]:
-                put()
-        for b in range(1, C):
-            ts(blk("mk", b), v("tau"), c("par", 96 + b), ALU.is_lt)
+            x_low(Xc, v("B6"), 0, 512)
+            gat("A", ve(Xc, M), v("B6", 0, E))
+            x_up(Xc, E, 2 * E)
+            swap("aX%d" % (r - 1), ve(Xc, E), ve(Xc, M), ve(Xc, V), ve(Xc, ext_last(rank)), ve(Xc, ext_last(rank - 1)))
+            gat("A", ve(Xc, M + E), v("B6", E, 2 * E))
+            for a, b, bank in ((512, 1024, "B4"), (1024, 1536, "B2"), (1536, M, "B3")):
+                x_low(Xc, v(bank, 0, b - a), a, b)
+        ts(v("par", 96, 97 + C), v("B7", 16, 17 + C), -896.25, ALU.add)
+        act(v("par", 112, 113 + C), v("B7", 16, 17 + C), AF.Identity, bias=c("col", 11 if last else 10))
         for b in range(1, C + 1):
-            ts(v("t1", 112 * b, 112 * b + 112), v("uu"), c("bF", b), ALU.is_ge, c("par", 15 + b), ALU.mult)
-        mm(v("pO", 0, K), IB, v("ones"), True)
-        for b in range(1, C):
-            mm(v("pO", 0, K), IB, blk("mk", b), False, b == C - 1)
-        mm(v("pS", 64, 176), v("i16"), v("uu"), True)
+            ts(v("te", HK * b, HK * b + HK), v("uu"), c("par", 96 + b), ALU.is_gt, c("par", 15 + b), ALU.mult)
+        mm(v("B7", 64, 176), I16, v("uu"), True)
         for b in range(1, C + 1):
-            mm(v("pS", 64, 176), v("i16"), v("t1", 112 * b, 112 * b + 112), False, b == C)
-        cp(blk("so", r), v("pO", 0, K))
-        both("aO%d" % r, blk("so", r), blk("soL", r), blk("soR", r))
-        cp(v("evI"), v("pS", 64, 176))
-        tt(v("sk"), blk("so", r), v("keep"), ALU.mult)
+            mm(v("B7", 64, 176), I16, v("te", HK * b, HK * b + HK), False, b == C)
+        ts(v("evI"), v("B7", 64, 176), -0.5, ALU.add)
         ts(v("evJ"), v("evI"), 1, ALU.bitwise_and)
-        tt(v("cS", 112, K), v("cV", 112, K), v("cA", 112, K), ALU.add)
-        tt(v("cS", 0, 112), v("cV", 0, 112), v("cA", 0, 112), ALU.add)
-        ts(v("off", 112, K), v("cS", 112, K), -63.75, ALU.add)
-        ts(v("off", 0, 112), v("cS", 0, 112), -63.75, ALU.add)
+        tt(v("cL", 0, ROT), v("cV", K - ROT, K), v("cA", K - ROT, K), ALU.add)
+        tt(v("cL", ROT, 114), v("cV", HK, HK + 96), v("cA", HK, HK + 96), ALU.add)
+        ts(v("oL", 0, HK), v("cL", 0, HK), -63.75, ALU.add)
+        tt(v("cU", 0, ROT), v("cV", HK - ROT, HK), v("cA", HK - ROT, HK), ALU.add)
+        tt(v("cU", ROT, 114), v("cV", 0, 96), v("cA", 0, 96), ALU.add)
+        ts(v("oU", 0, 114), v("cU", 0, 114), -63.75, ALU.add)
+        mm(v("B0", 0, HK), w("band", 0), v("cL", 0, HK), True)
+        mm(v("B0", 0, HK), w("band", 128), v("cL", 1, HK + 1), False, True)
         if not last:
             dma("S", [(row("winA", 0, 0, WID), v("zero")), (row("winV", 0, 0, WID), v("zero"))])
-        mm(v("pA", 128, 240), w("band", 0), v("cS", 112, K), True)
-        mm(v("pA", 128, 239), w("band", 128), v("cS", 113, K), False, True)
-        mm(v("pL", 0, 112), v("i32"), v("cS", 112, K), True)
-        mm(v("pS", 0, K), IB, v("sk"), True)
+        if r > 0:
+            x_up(Xc, 0, E)
+            for a, b, bank in ((512, 1024, "B4"), (1024, 1536, "B2"), (1536, M, "B3")):
+                gat("A", v(Xc, M + a, M + b), v(bank, 0, b - a))
+                x_up(Xc, a, b)
+        lag[0] = 60
+        for b in range(1, C):
+            act(blk("mo", b), v("kio", 0, K) if last else v("tI"), AF.Sign, bias=c("par", 112 + b), scale=-1.0 if last else -0.5)
+        for b in range(1, C):
+            mm(v("B7", 256, 256 + K), v("hb"), blk("mo", b), b == 1, b == C - 1)
+        act(v("so"), v("B7", 256, 256 + K), AF.Identity, bias=(C + 1) / 2.0)
+        lag[0] = 0
 
-        def met(a, b):
+        def low_names(a, b):
+            gat("A", v("nl", 16 * a, 16 * b), ind(Nc, "oL", a, b, n))
+
+        def check(a, b):
+            tt(v("eq", 16 * a, 16 * b), ind("hint" if r == 0 else Gc, "oU", a, b, n), v("nl", 16 * a, 16 * b), ALU.is_equal)
+
+        def mend(bank, bank2, a, b, piece):
             for i in range(16):
-                mm(v("pA", a, b), w("Z" if i else "U", 16 - i), v("eq", 16 * a + i, 16 * b, 16), i == 0)
-            e = min(b, 111)
-            mm(v("pA", a, e), w("U", 1), v("eq", 16 * a + 16, 16 * e + 1, 16), False, True)
+                mm(v(bank, a, b), w("Z" if i else "U", 16 - i), v("eq", 16 * a + i, 16 * b, 16), i == 0)
+            e = min(b, HK - 1)
+            mm(v(bank, a, e), w("U", 1), v("eq", 16 * a + 16, 16 * e + 1, 16), False, e == b)
+            if e < b:
+                mm(v(bank, e, b), w("U", 1), v("eq", 0, 1), False, True)
+            p0, p1 = piece
+            mm(v(bank2, p0, p1), v("i32"), v("cL", p0, p1), True)
+            ts(v("fl", a, b), v(bank, a, b), 0.5, ALU.is_gt)
+            tt(v("pp", a, b), v("fl", a, b), v("Dp", a, b), ALU.mult)
+            if b == HK:
+                cp(v("pp", 112, 114), v("pp", 0, 2))
+            mm(v(bank2, p0, p1), w("band", 256), v("pp", p0, p1))
+            mm(v(bank2, p0, p1), w("band", 384), v("pp", p0 - 1, p1 - 1), False, True)
+            ts(v("o2", p0, p1), v(bank2, p0, p1), -63.75, ALU.add)
 
-        for j in range(7):
-            gat("A", ve("nl", E * j), ind(Nc, n, "off", 112 + 16 * j, 128 + 16 * j))
-        for j in range(7):
-            tt(ve("eq", E * j), ind(Gc, n, "off", 16 * j, 16 * j + 16), ve("nl", E * j), ALU.is_equal)
-            if j == 0:
-                tt(v("Dp"), v("pA", 128, 240), v("evJ"), ALU.mult)
-            if j == 3:
-                met(0, 63)
-        met(63, 112)
-        if not last:
-            dma("S", [(row(Gc, 15 - r, 0, n), row(Nc, 0, 0, n))])
-        for a, b in ((0, 16), (96, 112), (16, 56), (56, 96)):
-            gat("A", v(Xn, 16 * a, 16 * b), ind(Xc, n, "off", a, b))
-        if last:
-            land_first, land_last = (lambda k: ve("nland", 0)), (lambda k: ve("nland", E))
-            dma("S", [(v("yx", lo, 1024), v(Xn, lo, 1024)), (v("yx", 1536, M), v(Xn, 1536, M))])
-        else:
-            land_first, land_last = (lambda k, x=Nn: ve(x, ext_first(k))), (lambda k, x=Nn: ve(x, ext_last(k)))
-        if left is not None:
-            gat("V", ve("nend", 0), ind(Nc, n, "off", 0, 16))
-            send("aN%d" % r, (ve("nend", 0), land_last(rank - 1)), None)
-        recv("aN%d" % r, None, land_last(rank))
-        ts(v("fl"), v("pA", 0, 112), 0.5, ALU.is_gt)
-        tt(v("pp"), v("fl"), v("Dp"), ALU.mult)
-        mm(v("pL", 0, 112), w("band", 256), v("pp"))
-        mm(v("pL", 1, 112), w("band", 384), v("pp", 0, 111), False, True)
-        ts(v("off2"), v("pL", 0, 112), -63.75, ALU.add)
-        from_ends("soL", "soR", r * K, False)
+        def kc(a):
+            return 16 * (a - 2)
+
+        def uppers(a, b):
+            gat("A", v(Xn, kc(a), kc(b)), ind(Xc, "oU", a, b, n))
 
         def diff(a, b):
-            tt(v("dd", 16 * a, 16 * b), ind(Xc, n, "off2", a, b), v(Xn, 16 * a, 16 * b), ALU.subtract)
+            tt(v(Xn, M + kc(a), M + kc(b)), ind(Xc, "o2", a, b, n), v(Xn, kc(a), kc(b)), ALU.subtract)
+
+        def greater(a, b):
+            ts(v("gs", a, b), v(Xn, M + a, M + b), 0.5, ALU.is_gt)
 
         def sign(a, b, eng):
             if eng == "V":
-                ts(v("sg", 16 * a, 16 * b), v("dd", 16 * a, 16 * b), 1.0, ALU.min, -1.0, ALU.max)
+                ts(v("gs", M + kc(a), M + kc(b)), v(Xn, M + kc(a), M + kc(b)), 1.0, ALU.min, -1.0, ALU.max)
             else:
-                act(v("sg", 16 * a, 16 * b), v("dd", 16 * a, 16 * b), AF.Sign)
+                act(v("gs", M + kc(a), M + kc(b)), v(Xn, M + kc(a), M + kc(b)), AF.Sign)
 
-        def greater(a, b):
-            ts(v("gt", 16 * a, 16 * b), v("dd", 16 * a, 16 * b), 0.5, ALU.is_gt)
+        def wins_list(bank, a, b, o):
+            for i in range(16):
+                mm(v(bank, o, o + b - a), w("U", 16 - i), v("gs", M + kc(a) + i, M + kc(b), 16), i == 0, i == 15)
 
-        def wins(i, a, b, name, start=False, stop=False, bank="pW"):
-            mm(v(bank, a, b), w(name, 16 - i), v("sg", K * i + a, K * i + b), start, stop)
+        def wins(i, a, b, name, bank, start=False, stop=False):
+            t = K * i + a
+            o = t + E if t < 1536 else t - 1536
+            mm(v(bank, a, b), w("U", 8 - i) if name == "Yl" else w(name, 16 - i), v("gs", M + o, M + o + b - a), start, stop)
 
-        def names(eng, offs, a, b):
-            o = M if offs == "off2" else 0
-            gat(eng, v(Gn, o + 16 * a, o + 16 * b), ind(Nc if last else Gc, n, offs, a, b))
+        def hist(out, offs, a, b):
+            gat("A", out, ind(Gc, offs, a, b, n))
 
-        def last_names():
-            if right is not None:
-                send("aM%d" % r, None, (ve("nend", E), land_first(rank + 1)))
-            recv("aM%d" % r, land_first(rank), None)
+        def upper_ends():
+            hist(v(Gn, 0, 512), "oU", *PE_)
+            swap("aG%d" % r, ve(Gn, E), ve(Gn, 0), ve("pland", pl), ve(Gn, ext_last(rank)), ve(Gn, ext_last(rank - 1)))
 
-        def end_results():
-            act(blk("sE", r), v("pT", 0, K), AF.Sign)
-            both("aS%d" % r, blk("sE", r), blk("sinL", r), blk("sinR", r))
-            yf = "Y" if left is None else "Yl"
-            yl = "Y" if right is None else "Yu"
-            wins(0, 0, K, yf, True)
-            wins(1, 0, 32, yf)
-            wins(6, 192, K, yl)
-            wins(7, 0, K, yl)
-
-        if right is not None:
-            gat("A", ve("nend", E), ind(Nc, n, "off2", 96, 112))
-        if last:
-            last_names()
-        diff(0, 16)
-        diff(96, 112)
-        sign(0, 16, "V")
-        sign(96, 112, "V")
-        wins(0, 0, K, "Yu", True, bank="pT")
-        wins(1, 0, 32, "Yu", bank="pT")
-        wins(6, 192, K, "Yl", bank="pT")
-        wins(7, 0, K, "Yl", False, True, bank="pT")
+        for a, b in CP:
+            low_names(a, b)
+        if r == 0:
+            upper_ends()
+        for piece in (PE_, PM1, PM2):
+            uppers(*piece)
+        for a, b in CP:
+            check(a, b)
+            if b == 36:
+                tt(v("Dp"), v("B0", 0, HK), v("evJ"), ALU.mult)
+            if a == 36:
+                mend("B1", "B2", 0, 34, PE_)
+            if a == 74:
+                mend("B3", "B4", 34, 72, PM1)
+        if r == 1:
+            dma("S", [(row(Gc, rho, 0, n), row(Nc, 0, 0, n))])
+        diff(*PE_)
+        sign(*PE_, "V")
         if not last:
-            names("A", "off", 0, 16)
-            end_results()
-            last_names()
-            for a, b in ((16, 42), (42, 56), (56, 70), (70, 84), (84, 96)):
-                diff(a, b)
-                sign(a, b, "A")
-            wins(1, 32, K, "Y")
-            for i in (2, 3, 4, 5):
-                wins(i, 0, K, "Y")
-            wins(6, 0, 192, "Y", False, True)
-            from_ends("sinL", "sinR", r * K, True)
-            greater(0, 56)
-            ts(v("cl"), v("pW", 0, K), 1.0, ALU.min, -1.0, ALU.max)
-            greater(56, 112)
-            tt(v("s"), v("pS", 0, K), v("cl"), ALU.add)
-            names("A", "off2", 0, 112)
-            names("A", "off", 16, 112)
-            dma("S", [(row(Nn, 0, 0, V), row(Gn, 15 - r, 0, V))])
-            dma("S", [(row(Gn, 15 - r, 0, M), row(Nn, 0, M, V)), (row(Gn, 15 - r, M, V), row(Nn, 0, 0, M))])
-            dma("S", [(row(Nn, j, lo, hi), row(Nn, 0, lo, hi)) for j in range(1, 16)])
-            ops[-1]["beside"] = True
-            swap_ends("aG%d" % r, Gn)
+            wins_list("B7", 2, 34, 0)
+        mend("B5", "B6", 72, HK, PM2)
+        if not last:
+            sn = "s%d" % (r + 1)
+            diff(34, 54)
+            act(v("cl", 96, HK), v("B7", 0, 16), AF.Sign)
+            act(v("cl", 0, 16), v("B7", 16, 32), AF.Sign)
+            if hasr:
+                tt(v("sx", 16, 32), v("so", K - 16, K), v("cl", 96, HK), ALU.add)
+            if hasl:
+                tt(v("sx", 0, 16), v("so", 0, 16), v("cl", 0, 16), ALU.subtract)
+            swap("aS%d" % r, v("sx", 0, 16), v("sx", 16, 32), v(sn, 0, 16), v(sn, K - 16, K))
+            diff(54, 72)
+            sign(*PM1, "A")
+            wins_list("B0", 34, 72, 16)
+            diff(72, 94)
+            sign(72, 94, "A")
+            diff(94, 114)
+            sign(94, 114, "V")
+            wins_list("B0", 72, 114, 54)
+            ts(v("cl", 16, 96), v("B0", 16, 96), 1.0, ALU.min, -1.0, ALU.max)
+            tt(v(sn, lo // 16, HK), v("so", lo // 16, HK), v("cl", lo // 16, HK), ALU.subtract)
+            tt(v(sn, HK, hi // 16), v("so", HK, hi // 16), v("cl", 0, hi // 16 - HK), ALU.add)
+            if r == 0:
+                ts(v("h16"), v("rel"), 0.0, ALU.is_equal, 0.5, ALU.mult)
+                lag[0] = 300
+                tt(v("Y", 8, 144), v("U", 0, 136), v("U", 8, 144), ALU.add)
+                lag[0] = 0
+            if r == 1:
+                upper_ends()
+            hist(v(Gn, M, M + 512), "o2", *PE_)
+            swap("aP%d" % r, ve(Gn, M + E), ve(Gn, M), ve(Gn, V), ve("pland", pl + E))
+            if r == 0:
+                for s in SHIFTS:
+                    pick(shift(s), v("blk1"), ALU.is_equal, 0.0, -s)
+            lag[0] = 60
+            for a in range(0, M, 448):
+                greater(a, a + 448)
+            lag[0] = 0
+            for offs, o in (("o2", M), ("oU", 0)):
+                for a, b in ((34, 74), (74, 114)):
+                    hist(v(Gn, o + kc(a), o + kc(b)), offs, a, b)
+            dma("S", [(row(Nn, 0, 0, wid), row(Gn, rho, 0, wid))])
+            fix = [(row(Gn, rho, 0, M), row(Nn, 0, M, V)), (row(Gn, rho, M, V), row(Nn, 0, 0, M))]
+            if hasl:
+                fix.append((row(Gn, rho, V, V + E), row("pland", rho, pl, pl + E)))
+            if hasr:
+                fix.append((row(Gn, rho, ext_last(rank), wid), row("pland", rho, pl + E, pl + 2 * E)))
+            dma("S", [(row(Nn, j, 0, wid), row(Nn, 0, 0, wid)) for j in range(1, 16)])
+            dma("S", fix)
         else:
-            top = (hi - M) // 16
-            greater(0, 16)
-            greater(96, 112)
-            put = x_lower(Xn, 1536, M, "A", True, "pX0")
-            if left is not None:
-                tt(v("xend"), ve(Xn, 0), ve("gt", 0), ALU.add)
-            names("A", "off", lo // 16, 56)
-            put()
-            send("aX%d" % r, (v("xend"), ve("xland", E)), (ve(Xn, V - E), ve("xland", 0)))
-            recv("aX%d" % r, ve("xland", 0), ve("xland", E))
-            end_results()
-            names("A", "off", 56, 112)
-            dma("S", [(v("yn", lo, M), row(Gn, 0, lo, M))])
-            puts = []
-            for j, (a, b) in enumerate(((16, 32), (32, 64), (64, 80), (80, 96))):
-                diff(a, b)
-                sign(a, b, "V")
+            def names(eng, out, offs, a, b):
+                gat(eng, out, ind(Nc, offs, a, b, n))
+
+            def boards(bank, a, b):
                 greater(a, b)
-                a = a if j else 0
-                put = x_lower(Xn, 16 * a, 16 * b, "A" if j < 3 else "V", True, ("pX1", "pX0", "pA", "pL")[j])
-                if j < 2:
-                    put()
-                else:
-                    puts.append(put)
-                if j == 1:
-                    dma("S", [(v("yx", M, M + 1024), v(Xn, M, M + 1024))])
-                    dma("G", [(v("yx", lo, 1024), v("gt", lo, 1024)), (v("yx", 1536, M), v("gt", 1536, M))], True)
-                    wins(1, 32, K, "Y")
-                    wins(2, 0, K, "Y")
-                    wins(3, 0, K, "Y")
-            tt(v("eq", 0, 512), v(Xn, 1024, 1536), v("gt", 1024, 1536), ALU.add)
-            wins(4, 0, K, "Y")
-            wins(5, 0, K, "Y")
-            wins(6, 0, 192, "Y", False, True)
-            from_ends("sinL", "sinR", r * K, True)
-            hm = top - 26
-            puts[0]()
-            puts[1]()
-            names("A", "off2", 0, hm)
-            ts(v("cl"), v("pW", 0, K), 1.0, ALU.min, -1.0, ALU.max)
-            names("V", "off2", hm, hm + 8)
-            tt(v("sf"), v("pS", 0, K), v("cl"), ALU.add)
-            names("V", "off2", hm + 8, top)
+                tt(v("eq", a, b), v(Xn, a, b), v("gs", a, b), ALU.add)
+                px = v(bank, 0, b - a)
+                mm(px, IB, v(Xn, M + a, M + b), True)
+                mm(px, v("ineg"), v("gs", M + a, M + b))
+                mm(px, IB, v("eq", a, b), False, True)
+                gat("A", v("xo", a, b), px)
+
+            def middle(bank, a, b):
+                boards(bank, a, b)
+                dma("S", [(v("yx", a - E, b - E), v("eq", a, b)), (v("yx", M + a - E, M + b - E), v("xo", a, b))])
+
+            yf = "Yl" if hasl else "Y"
+            yl = "U" if hasr else "Y"
+            wins(0, 0, K, "U", "B7", True)
+            wins(1, 0, 32, "U", "B7")
+            wins(6, 192, K, "Yl", "B7")
+            wins(7, 0, K, "Yl", "B7", False, True)
+            act(v("cl"), v("B7", 0, K), AF.Sign, scale=c("col", 8))
+            tt(v("sE"), v("cl"), v("so"), ALU.add)
+            swap("aS2", v("sE"), v("sE"), v("sinL"), v("sinR"))
+            names("A", ve(Gn, V - E), "o2", 2, 18)
+            names("A", ve(Gn, 0), "oU", 18, 34)
+            swap("aN", ve(Gn, 0), ve(Gn, V - E), ve("nland", 0), ve("nland", E))
+            boards("B2", 0, 512)
+            swap("aX2", ve("eq", E), ve("xo", 0), ve("xland", 0), ve("xland", E))
+            outs = [(ve("yx", 1536), ve("eq", 0)), (ve("yx", M), ve("xo", E))]
+            if not hasl:
+                outs.append((ve("yx", 0), ve("eq", E)))
+            if not hasr:
+                outs.append((ve("yx", V - E), ve("xo", 0)))
+            dma("S", outs)
+            diff(*PM1)
+            sign(*PM1, "A")
+            diff(72, 94)
+            middle("B3", 512, 1024)
+            sign(72, 94, "V")
+            diff(94, 114)
             ends = []
-            if left is not None:
+            if hasl:
                 ends += [(ve("yn", 0), row("nland", 0, 0, E)), (ve("yx", 0), ve("xland", 0))]
-            if right is not None:
+            if hasr:
                 ends += [(ve("yn", V - E), row("nland", 0, E, 2 * E)), (ve("yx", V - E), ve("xland", E))]
             dma("S", ends)
-            dma("S", [(v("yx", 1024, 1536), v("eq", 0, 512))])
-            dma("S", [(v("yx", M + 1024, hi), v(Xn, M + 1024, hi))])
+            sign(94, 114, "V")
+            middle("B4", 1024, 1472)
+            middle("B5", 1472, M)
+            mm(v("B1", 0, K), w("dk", 128), v("so"), True)
+            if hasl:
+                mm(v("B1", 0, 32), w("dn", 0), v("so", 0, 32))
+            if hasr:
+                mm(v("B1", 192, K), w("dn", 128), v("so", 192, K))
+            from_ends("sinL", "sinR")
+            wins(0, 0, K, yf, "B0", True)
+            wins(1, 0, 32, yf, "B0")
+            wins(6, 192, K, yl, "B0")
+            wins(7, 0, K, yl, "B0")
+            wins(1, 32, K, "Y", "B0")
+            for i in (2, 3, 4, 5):
+                wins(i, 0, K, "Y", "B0")
+            wins(6, 0, 192, "Y", "B0", False, True)
+            act(v("cl"), v("B0", 0, K), AF.Sign, scale=c("col", 8))
+            tt(v("sf"), v("B1", 0, K), v("cl"), ALU.add)
             dma("S", [(v("ys"), v("sf"))])
+            names("A", ve(Gn, 1536), "oU", 2, 18)
+            for a, b in ((34, 60), (60, 88), (88, 114)):
+                names("A", v(Gn, 16 * (a - ROT), 16 * (b - ROT)), "oU", a, b)
+            dma("A", [(v("yn", lo, M), row(Gn, 0, lo, M))])
+            names("V", v(Gn, M, 16 * (NS - ROT) + M), "o2", 18, NS)
+            names("A", v(Gn, 16 * (NS - ROT) + M, V - E), "o2", NS, 114)
             dma("A", [(v("yn", M, hi), row(Gn, 0, M, hi))])
-    emit(g, T, Q, ops)
+    emit(g, T, Q, arrange(ops))
+
+
+def meets(a, b):
+    for n1, l1, h1, r1 in a:
+        for n2, l2, h2, r2 in b:
+            if n1 == n2 and l1 < h2 and l2 < h1 and (r1 is None or r2 is None or r1 == r2):
+                return True
+    return False
+
+
+def ordered(o, op):
+    if o["eng"] == "P" and op["eng"] == "P":
+        return bool(op["bank"] & o["bank"])
+    return (meets(op["R"], o["W"]) or meets(op["W"], o["W"]) or meets(op["W"], o["R"])
+            or (o["eng"] != op["eng"] and bool(op["bank"] & o["bank"])))
+
+
+def arrange(ops):
+    n = len(ops)
+    by, sent, before, todo = {}, {}, {}, {}
+    for k, op in enumerate(ops):
+        op["names"] = set(x[0] for x in op["R"] + op["W"])
+        op["bank"] = set(x for x in op["names"] if SCRATCH.get(x, ("",))[0] == "psum")
+        cand = set()
+        for x in op["names"]:
+            cand.update(by.get(x, ()))
+        dep = [j for j in cand if ordered(ops[j], op)]
+        soft = [before[op["eng"]]] if (op["eng"] in ("S", "G") or op["kind"] == "d") and op["eng"] in before else []
+        before[op["eng"]] = k
+        if "pair" in op:
+            sent[op["pair"]] = k
+        if op["kind"] == "r":
+            dep.append(sent[op["sem"]])
+        for x in op["names"]:
+            by.setdefault(x, []).append(k)
+        op["nxt"], op["behind"] = [], []
+        for j in dep:
+            ops[j]["nxt"].append(k)
+        for j in soft:
+            ops[j]["behind"].append(k)
+        cst = op["cost"]
+        op["hold"], op["span"] = (cst[0], sum(cst)) if op["kind"] == "d" else (0.0, 0.4) if op["kind"] == "r" else (cst, cst)
+        op["open"], op["known"] = set(dep) | set(soft), 0.0
+        todo.setdefault(op["eng"], []).append(k)
+    for k in range(n - 1, -1, -1):
+        ops[k]["key"] = min([ops[k]["key"]] + [ops[j]["key"] - 0.01 for j in ops[k]["nxt"] + ops[k]["behind"]])
+    for mine in todo.values():
+        mine.sort(key=lambda k: (ops[k]["key"], k))
+    free = {e: 0.0 for e in todo}
+    wire, first, out = 0.0, True, []
+    while len(out) < n:
+        memo = {}
+
+        def ready(k, depth):
+            if k not in memo:
+                op = ops[k]
+                t = max(free[op["eng"]], op["known"])
+                if op["open"]:
+                    j = max(op["open"])
+                    t = max(t, ready(j, depth + 1) + ops[j]["span"] + WAKE) if depth < DEPTH else t + 2.0
+                memo[k] = t
+            return memo[k]
+
+        best = None
+        for e, mine in todo.items():
+            bound = 1e9
+            for k in mine[:AHEAD.get(e, 4)]:
+                t = ready(k, 0)
+                if not ops[k]["open"] and t + ops[k]["hold"] <= bound + SLACK and (best is None or (t, ops[k]["key"]) < best[:2]):
+                    best = (t, ops[k]["key"], k)
+                bound = min(bound, t)
+                if bound + SLACK <= free[e] + 0.03:
+                    break
+        at, _key, k = best
+        op = ops[k]
+        todo[op["eng"]].remove(k)
+        out.append(k)
+        hold = op["hold"]
+        if "pair" in op and first:
+            first = False
+            hold += 2.5
+        if op["kind"] != "r":
+            free[op["eng"]] = at + hold
+        if op["kind"] == "d":
+            wire = max(wire, at + hold + op["cost"][1] / 2) + op["cost"][2]
+            end = wire + op["cost"][1] / 2
+        else:
+            end = at + op["span"]
+        for j in op["nxt"]:
+            ops[j]["open"].discard(k)
+            ops[j]["known"] = max(ops[j]["known"], end + (0.0 if op["eng"] == "P" and ops[j]["eng"] == "P" else WAKE))
+        for j in op["behind"]:
+            ops[j]["open"].discard(k)
+            ops[j]["known"] = max(ops[j]["known"], at + hold)
+    return [ops[k] for k in out]
 
 
 def emit(g, T, Q, ops):
-    def meets(a, b):
-        for n1, l1, h1 in a:
-            for n2, l2, h2 in b:
-                if n1 == n2 and l1 < h2 and l2 < h1:
-                    return True
-        return False
-
-    for op in ops:
-        op["names"] = set(x[0] for x in op["R"] + op["W"])
-        op["bank"] = set(x for x in op["names"] if SCRATCH.get(x, ("",))[0] == "psum")
     know = {e: {} for e in Q}
     pos = {e: 0 for e in Q}
     nd = 0
@@ -590,10 +743,9 @@ def emit(g, T, Q, ops):
             o = ops[j]
             if know[e].get(o["tok"][0], 0) >= o["tok"][1] or not (op["names"] & o["names"]):
                 continue
-            if (o["eng"] == "P" and e == "P") or (op.get("beside") and j == k - 1):
+            if o["eng"] == "P" and e == "P":
                 continue
-            if (meets(op["R"], o["W"]) or meets(op["W"], o["W"]) or meets(op["W"], o["R"])
-                    or (o["eng"] != e and op["bank"] & o["bank"])):
+            if ordered(o, op):
                 waits.append(j)
                 o["seen"] = True
                 for t, x in o["clock"].items():

from concourse.bass import DstId, RemoteDMATransfer
from concourse.mybir import AluOpType, ActivationFunctionType

ALU, AF = AluOpType, ActivationFunctionType
V, M, E, RO = 3584, 1792, 256, 3
K, HK = 224, 112
WID = 4096
F, B, H, I, U16 = "float32", "bfloat16", "float16", "int32", "uint16"
SCRATCH = {}
for _n, _d, _names in (
        (V, I, "hint"), (V, F, "val"), (V, B, "gs"), (WID, B, "X0 X1"), (WID, F, "winV winA G0 G1 N0 N1"), (M, F, "nl"),
        (M, B, "eq xo"), (2 * E, F, "nland"), (4 * E, F, "pland"), (2 * E, B, "xland"),
        (K, I, "sci nmi Ti Tj"), (K, F, "nmf sf tI"), (K, B, "s0 s1 s2 cl so sE sinL sinR"),
        (8 * K, B, "mk mo"), (8 * K + 16, B, "q"), (8 * K, H, "t1 t2"), (4 * K, B, "t3"), (9 * HK, H, "te"),
        (K, H, "pz fz"), (32, I, "bI"), (128, F, "par cU cL pp jt i32 bp bn"), (K, U16, "soff"), (256, F, "cV cA kio zero"),
        (128, U16, "oU oL o2"), (HK, I, "evI evJ"), (HK, F, "Dp fl"), (32, B, "sx"), (4, I, "pidx"), (16, F, "col"),
        (128, B, "rel triL triU half blk1 triB ib i896 ineg hb"), (144, B, "relj a32 b32 Z U Y"), (3 * 128, B, "ab"),
        (256, B, "dk dn"), (4 * 128, B, "sh"), (128, H, "h16 i16"), (4 * 128, F, "band"), (HK, H, "uu"), (48, B, "cst")):
    for _x in _names.split():
        SCRATCH[_x] = ("sbuf", [128, _n], _d)
for _k in range(8):
    SCRATCH["B%d" % _k] = ("psum", [128, 512], F)
NDMA = 110
SEMAPHORES = (["eV", "eA", "eP", "eG"] + ["d%d" % i for i in range(NDMA)]
              + ["%s%d" % (k, r) for k in ("aS", "aX") for r in range(RO)]
              + ["%s%d" % (k, r) for k in ("aG", "aP") for r in range(RO - 1)] + ["aN"])
KA = (146, 114, 114)
KG = 160
NS = 68
SHIFTS = (14, 15, -14, -15)
BIG = 1 << 20
CYC, PEC, GATH, SCAT, WAKE, RATE = 0.00083, 0.6, 1.25, 2.2, 0.13, 4.0e5
AHEAD, SLACK, DEPTH = {"V": 72, "A": 40, "P": 160}, 0.04, 24
ROT = 18
PE_, PM1, PM2 = (2, 34), (34, 72), (72, 114)
CP = ((0, 18), (18, 36), (36, 56), (56, 74), (74, 94), (94, HK))


def rank_program(g, core, T, topo):
    rank = T.rank_of(core)
    if rank is None:
        return
    nr = len(T.cores)
    left = T.cores[rank - 1] if rank > 0 else None
    right = T.cores[rank + 1] if rank + 1 < nr else None
    hasl, hasr = left is not None, right is not None
    lo = E if hasl else 0
    hi = V - E if hasr else V
    wid = V + E * (hasl + hasr)

    def ext_last(k):
        return V + (E if k > 0 else 0)

    Q = {"V": g.vector, "A": g.scalar, "P": g.tensor, "S": g.sync, "G": g}
    ops = []
    lag = [0]

    def v(name, a=None, b=None, st=None):
        if a is None:
            return (T[name][:], [(name, 0, BIG, None)], int(T[name].shape[1]))
        if st is None:
            return (T[name][:, a:b], [(name, a, b, None)], b - a)
        return (T[name][:, a:b:st], [(name, a, b, None)], len(range(a, b, st)))

    def ve(name, a):
        return v(name, a, a + E)

    def c(name, j):
        return v(name, j, j + 1)

    def w(name, o):
        return v(name, o, o + 128)

    def shift(s):
        return w("sh", 128 * SHIFTS.index(s))

    def row(name, r, a, b):
        return (T[name][r::16, a:b], [(name, a, b, r)], (b - a) // 16)

    def ind(name, offs, a, b, n):
        return (T[name][:, 0:n].indirect(T[offs][:, a:b]), [(name, 0, n, None), (offs, a, b, None)], 16 * (b - a))

    def blk(name, b, o=0, n=1):
        return v(name, o + b * K, o + (b + n) * K)

    def ap(x):
        return x[0] if isinstance(x, tuple) else x

    def regs(*xs):
        out = []
        for x in xs:
            if isinstance(x, tuple):
                out += x[1]
        return out

    def add(eng, kind, fn, R, W, n=1, sem=None, cost=0.0):
        ops.append({"eng": eng, "kind": kind, "fn": fn, "R": R, "W": W, "n": n, "sem": sem, "cost": cost, "key": len(ops) + lag[0]})

    def wide(x):
        return SCRATCH[x[1][0][0]][2] in (F, I) if x[1][0][0] in SCRATCH else x[1][0][0] not in ("x", "yx")

    def cyc(out, *ins, both=False, fix=0.0):
        if len(out[1]) > 1:
            return 0.06 + CYC * SCAT * out[2]
        if ins and len(ins[0][1]) > 1:
            return 0.06 + CYC * GATH * out[2]
        k = 1.0 if fix or any(wide(x) for x in (out,) + ins) else 0.5
        if both and not any(SCRATCH[x[1][0][0]][0] == "psum" for x in ins):
            k *= 2
        return (fix or 0.05) + CYC * max(64, k * out[2])

    def ts(out, in0, s1, op0, s2=None, op1=None):
        if op1 is None:
            add("V", "c", lambda: g.vector.tensor_scalar(out[0], in0[0], ap(s1), None, op0), regs(in0, s1), out[1],
                cost=cyc(out, in0))
        else:
            add("V", "c", lambda: g.vector.tensor_scalar(out[0], in0[0], ap(s1), ap(s2), op0, op1), regs(in0, s1, s2), out[1],
                cost=cyc(out, in0))

    def tt(out, a, b, op):
        add("V", "c", lambda: g.vector.tensor_tensor(out[0], a[0], b[0], op), regs(a, b), out[1], cost=cyc(out, a, b, both=True))

    def cp(out, a):
        add("V", "c", lambda: g.vector.tensor_copy(out[0], a[0]), regs(a) + out[1][1:], out[1][:1], cost=cyc(out, a))

    def ms(out, x):
        add("V", "c", lambda: g.vector.memset(out[0], x), [], out[1], cost=cyc(out))

    def scan(out, a, init=0.0):
        add("V", "c", lambda: g.vector.tensor_tensor_scan(out[0], a[0], a[0], ap(init), ALU.add, ALU.max), regs(a, init), out[1],
            cost=cyc(out, a))

    def act(out, a, func, bias=0.0, scale=1.0):
        if bias == 0.0 and scale == 1.0:
            add("A", "c", lambda: g.scalar.activation(out[0], a[0], func), regs(a) + out[1][1:], out[1][:1],
                cost=cyc(out, a, fix=0.06))
        else:
            add("A", "c", lambda: g.scalar.activation(out[0], a[0], func, bias=ap(bias), scale=ap(scale)),
                regs(a, bias, scale) + out[1][1:], out[1][:1], cost=cyc(out, a, fix=0.06) + (1.3 if func == AF.Silu else 0.0))

    def gat(eng, out, a):
        if eng == "V":
            cp(out, a)
        else:
            act(out, a, AF.Identity)

    def mm(out, l, r, start=False, stop=False):
        add("P", "c", lambda: g.tensor.matmul(out[0], l[0], r[0], start, stop), regs(l, r), out[1],
            cost=0.015 + CYC * PEC * max(64, r[2]) * (4 if wide(l) else 1))

    def iota(out, pat, base, cm, flag=True):
        if flag:
            add("G", "c", lambda: g.iota(out[0], pat, base, cm, allow_small_or_imprecise_dtypes=True), [], out[1],
                cost=0.13 + 2 * CYC * out[2])
        else:
            add("G", "c", lambda: g.iota(out[0], pat, base, cm), [], out[1], cost=0.13)

    def pick(out, a, op, fill, base, pat=((1, 128),), cm=-1):
        add("G", "c", lambda: g.affine_select(out[0], a[0], [list(x) for x in pat], op, fill, base, cm), a[1], out[1],
            cost=0.17 + 2 * CYC * out[2])

    def dma(eng, pairs):
        def fn(sem):
            for o, i in pairs:
                Q[eng].dma_start(o[0], i[0]).then_inc(sem, 16)
        R, W, nb = [], [], 0
        for o, i in pairs:
            R += i[1]
            W += o[1]
            x = o if o[1][0][0] in SCRATCH else i
            nb += 128 * x[2] * (4 if wide(x) else 2)
        add(eng, "d", fn, R, W, 16 * len(pairs), cost=(0.06 * len(pairs), 1.5, nb / RATE))

    def half_mask(src, dst):
        en = topo.engines(src, dst)
        h = len(en) // 2
        part = en[h:] if T.rank_of(dst) > T.rank_of(src) else en[:h]
        return sum(1 << e for e in part), len(part)

    def swap(sem, first, last, land_first, land_last, at_left=None):
        tr, R, W, cnt, got = [], [], [], 0, 0
        for other, src, there, here in ((left, first, at_left or land_last, land_first), (right, last, land_first, land_last)):
            if other is None:
                continue
            rid, pid, _se = topo.addr(other)
            mask, k = half_mask(core, other)
            tr.append(RemoteDMATransfer(dst_ids=[DstId(rid=rid, pnc=pid)], dma_engine_mask=mask, remote_sem=T.sem[sem],
                                        src=src[0], dst=there[0]))
            R += src[1]
            W += here[1]
            cnt += k
            got += half_mask(other, core)[1]
        nb = len(tr) * 128 * first[2] * (4 if wide(first) else 2)
        add("G", "d", lambda s: g.remote_dma_fused(tr, local_sem=s), R, [], cnt, cost=(0.4, 1.6, nb / RATE))
        ops[-1]["pair"] = sem
        add(None, "r", None, [], W, got, sem)

    IB, I16 = v("ib"), v("i16")
    dma("S", [(v("sci"), v("sc"))])
    dma("S", [(v("nmi"), v("nm"))])
    iota(c("pidx", 0), [[0, 1]], 0, 1, False)
    iota(v("jt"), [[64, 8], [1, 16]], 0, 0)
    iota(v("cst"), [[1792, 3], [0, 16]], -1792, 0)
    iota(v("q", 0, 16), [[0, 16]], 0, 0)
    ka = KA[0]
    iota(v("val", 0, 16 * (K - KG)), [[1, K - KG], [K, 16]], 64, 0)
    iota(v("val", 16 * (K - KG), 16 * ka), [[1, ka - K + KG], [K, 16]], 64 + K - KG, 0)
    iota(v("val", 16 * ka, 16 * KG), [[1, KG - ka], [K, 16]], 64 + ka, 0)
    iota(v("kio"), [[1, 256]], 0, 0)
    iota(v("tI"), [[1, 2], [32, HK]], 0, 2)
    ms(v("zero"), 0.0)
    dma("S", [(row("winA", 0, 0, WID), v("zero")), (row("winV", 0, 0, WID), v("zero"))])
    dma("S", [(v("hint", 0, M), v("hi", 0, M))])
    ts(c("pidx", 1), c("pidx", 0), 15, ALU.bitwise_and)
    ts(c("pidx", 2), c("pidx", 0), 4, ALU.logical_shift_right)
    cp(c("col", 0), c("pidx", 1))
    ts(c("col", 1), c("pidx", 2), -64.0, ALU.mult)
    tt(c("col", 2), c("col", 0), c("col", 1), ALU.subtract)
    ts(v("rel"), v("jt"), c("col", 2), ALU.subtract)
    for j, bias in enumerate((0.0, -8.0, 8.0)):
        act(w("ab", 128 * j), v("rel"), AF.Abs, bias=bias)
    ts(IB, v("rel"), 0.0, ALU.is_equal)
    act(v("i896"), IB, AF.Silu, scale=896.0)
    act(v("val", 16 * KG, V), v("val", 0, 16 * (K - KG)), AF.Identity, bias=float(KG))
    ts(I16, v("rel"), 0.0, ALU.is_equal)
    ts(v("half"), w("ab", 0), 15.5, ALU.is_lt, 0.5, ALU.mult)
    ts(v("triL"), w("ab", 128), 7.5, ALU.is_lt)
    ts(v("triU"), w("ab", 256), 7.5, ALU.is_lt)
    cp(v("s0"), v("sci"))

    def counts(C, stop):
        e_all = v("q", 15, 16 + C * K, K)
        mm(v("B7", 16, 17 + C), v("half"), e_all)
        mm(v("B7", 32, 33 + C), v("half"), e_all, False, stop)

    def window_columns(bank, const, ka):
        for a, b in ((0, ka), (ka, K)):
            ts(v("Ti", a, b), v(bank, a, b), const, ALU.add, 4097.0, ALU.mult)
            ts(v("Tj", a, b), v("Ti", a, b), 4, ALU.logical_shift_right, 4095, ALU.bitwise_and)
            cp(v("soff", a, b), v("Tj", a, b))

    def sort_blocks(C):
        pT = v("B5", 0, K)
        mm(v("B7", 0, 48), IB, v("cst"), True)
        for b in range(C):
            ts(blk("mk", b), v("s0"), float(C - 1 - b), ALU.is_equal)
        scan(v("q", 16, 16 + C * K), v("mk", 0, C * K))
        cp(v("nmf"), v("nmi"))
        dma("S", [(row("N0", 0, 0, V), v("nmf"))])
        dma("S", [(v("hint", M, V), v("hi", M, V))])
        dma("S", [(row("N0", j, 0, V), row("N0", 0, 0, V)) for j in range(1, 16)])
        counts(C, False)
        mm(v("B7", 0, C), v("triL"), v("q", 15 + K, 16 + C * K, K))
        mm(v("B7", 0, C), v("triU"), v("q", 15, 16 + (C - 1) * K, K), False, True)

        def member(b, m):
            tt(blk("t3", b, 0, m), blk("mk", b, 0, m), blk("q", b, 16, m), ALU.mult)
            for j in range(b, b + m):
                mm(pT, IB, blk("t3", j), j == 0)

        def base(b):
            ts(blk("t1", b), blk("mk", b), c("par", b), ALU.mult)
            mm(pT, I16, blk("t1", b))

        member(0, 2)
        ts(v("bI"), v("B7", 16, 48), -0.25, ALU.add)
        member(2, 1)
        tt(v("par", 0, C), v("B7", 0, C), v("bI", 0, C), ALU.subtract)
        tt(v("par", 16, 16 + C), v("bI", 16, 16 + C), v("bI", 1, 1 + C), ALU.subtract)
        tt(v("par", 32, 32 + C), v("bI", 1, 1 + C), v("par", 0, C), ALU.subtract)
        base(0)
        tt(v("par", 64, 64 + C), v("par", 32, 32 + C), v("par", 16, 16 + C), ALU.subtract)
        ts(v("par", 48, 48 + C), v("par", 32, 32 + C), -1791.5, ALU.add, 0.5, ALU.max)
        ts(v("par", 80, 80 + C), v("par", 64, 64 + C), 0.5, ALU.add, 0.5, ALU.max)
        member(3, 1)
        for b in range(C - 1):
            act(blk("mo", b), blk("t3", b), AF.Sign, bias=c("par", 80 + b), scale=-1.0)
        for b in range(1, C):
            base(b)
        for b in range(C):
            ts(blk("t2", b), blk("t3", b), c("par", 48 + b), ALU.is_gt, c("par", 16 + b), ALU.mult)
            mm(pT, I16, blk("t2", b))
        for b in range(C - 1):
            mm(pT, v("i896"), blk("mo", b), False, b == C - 2)
        window_columns("B5", float(1791 - 896 * (C - 1)), KA[0])

    def sort_lists(C, s, ka):
        hc = C // 2
        mm(v("B7", 16, 48), v("ineg"), v("cst", 16, 48), True)
        for k in range(hc):
            for b in (2 * k, 2 * k + 1):
                ts(blk("mk", b), v(s), float(C - 1 - b), ALU.is_equal)
            scan(blk("q", 2 * k, 16, 2), blk("mk", 2 * k, 0, 2), c("q", 15 + 2 * k * K))
        counts(C, True)
        for j in range(hc):
            mm(v("B%d" % j, 0, 2 * K), v("blk1"), blk("q", 2 * j, 15, 2), True)
            mm(v("B%d" % j, 0, 2 * K), v("triB"), blk("mk", 2 * j, 0, 2), False, True)
        for j in range(hc):
            ts(blk("t1", 2 * j, 0, 2), v("B%d" % j, 0, 2 * K), -5888.0, ALU.add, -2048.0, ALU.max)
            if j == hc - 3:
                ts(v("bI"), v("B7", 16, 48), -0.25, ALU.add)
            if j == hc - 2:
                tt(v("par", 16, 16 + C), v("bI", 0, C), v("bI", 1, 1 + C), ALU.subtract)
                tt(v("par", 32, 32 + C), v("bI", 16, 16 + C), v("bI", 1, 1 + C), ALU.add)
            for b in (2 * j, 2 * j + 1):
                mm(v("B4", 0, K), I16, blk("t1", b), b == 0, b == C - 1)
        ts(v("pz"), v("B4", 0, K), 2048.0 * (C - 1), ALU.add)
        mm(v("B5", 0, K), v("h16"), v("pz"), True)
        for b in range(C):
            ts(blk("t2", b), v("pz"), c("par", 32 + b), ALU.is_ge, c("par", 16 + b), ALU.mult)
            mm(v("B5", 0, K), I16, blk("t2", b), False, b == C - 1)
        ts(v("fz"), v("B5", 0, K), -896.25, ALU.is_lt, 1792.0, ALU.mult)
        mm(v("B0", 0, K), I16, v("pz"), True)
        for b in range(C):
            mm(v("B0", 0, K), I16, blk("t2", b))
        mm(v("B0", 0, K), I16, v("fz"), False, True)
        window_columns("B0", 1792.0, ka)

    def x_low(X, px, a, b):
        mm(px, IB, v(X, a, b), True)
        mm(px, IB, v(X, M + a, M + b))
        mm(px, IB, v("gs", a, b))
        mm(px, v("ineg"), v("gs", M + a, M + b), False, True)

    def x_up(X, a, b):
        tt(v(X, a, b), v(X, a, b), v("gs", a, b), ALU.add)

    def from_ends(at_left, at_right):
        arr = []
        if hasr:
            arr += [(192, K, 14, v(at_right, 0, 32)), (0, 192, 15, v(at_right, 32, K))]
        if hasl:
            arr += [(0, 32, -14, v(at_left, 192, K)), (32, K, -15, v(at_left, 0, 192))]
        for j, (a, b, s, src) in enumerate(arr):
            mm(v("B1", a, b), shift(s), src, False, j == len(arr) - 1)

    for r in range(RO):
        C = 4 + 2 * r
        Gc, Nc, Xc = "G%d" % (r % 2), "N%d" % (r % 2), "X%d" % (r % 2)
        Gn, Nn, Xn = "G%d" % (1 - r % 2), "N%d" % (1 - r % 2), "X%d" % (1 - r % 2)
        last = r == RO - 1
        ka = KA[r]
        rho = 15 - r
        pl = 2 * E * r
        n = V if r == 0 else wid
        if r == 0:
            sort_blocks(C)
        else:
            sort_lists(C, "s%d" % r, ka)
        act(ind("winA", "soff", 0, ka, WID), v("val", 0, 16 * ka), AF.Silu)
        dma("A", [(v("cA"), row("winA", 0, 0, WID))])
        cp(ind("winV", "soff", ka, K, WID), v("val", 16 * ka, V))
        dma("S", [(v("cV"), row("winV", 0, 0, WID))])
        if r == 0:
            dma("A", [(v("X0", 0, V), v("x"))])
            act(v("bp"), v("half"), AF.Identity, scale=2.0)
            act(v("bn"), v("half"), AF.Identity, scale=-2.0)
            act(v("blk1"), v("half"), AF.Identity, scale=2.0)
            pick(w("band", 128), v("bp"), ALU.is_equal, 0.0, -15)
            pick(w("band", 384), v("bn"), ALU.is_equal, 0.0, 15)
            pick(v("bp"), v("bp"), ALU.is_equal, 0.0, 1)
            pick(v("bn"), v("bn"), ALU.is_equal, 0.0, -1)
            pick(w("band", 0), v("bp"), ALU.not_equal, -1.0, 0)
            pick(w("band", 256), v("bn"), ALU.not_equal, 1.0, 0)
            pick(v("triB"), v("triL"), ALU.not_equal, 4096.0, 0)
            inner = ((0, 8), (1, 16))
            pick(w("dk", 0), IB, ALU.not_equal, 0.0, 0 if hasl else 99, inner, 0)
            pick(w("dk", 128), w("dk", 0), ALU.not_equal, 0.0, -15 if hasr else 99, inner, 0)
            act(v("ineg"), IB, AF.Identity, scale=-1.0)
            pick(w("dn", 0), v("ineg"), ALU.is_equal, 0.0, -1, inner, 0)
            pick(w("dn", 128), v("ineg"), ALU.is_equal, 0.0, -14, inner, 0)
            for a, b, at in ((M + 1536, V, ext_last(rank) if hasr else M), (16 * ka, M + 1536, 16 * ka + E), (M, 16 * ka, M + E),
                             (1536, M, 0), (E, 1536, 2 * E), (0, E, V if hasl else E)):
                iota(v("val", a, b), [[1, b - a]], 64 + at, 0)
            cp(v("G0", 0, V), v("hint"))
            dma("S", [(row(Gc, rho, 0, V), row(Nc, 0, 0, V))])
            act(c("col", 9), c("col", 1), AF.Identity, bias=-16.0, scale=0.25)
            act(c("col", 3), c("col", 1), AF.Identity, bias=-895.0, scale=0.25)
            act(c("col", 8), c("col", 0), AF.Sign, bias=-7.5)
            act(c("col", 4), c("col", 0), AF.Identity, bias=895.5, scale=-224.0)
            act(c("col", 11), c("col", 8), AF.Identity, bias=c("col", 4), scale=895.75)
            act(c("col", 10), c("col", 1), AF.Identity, bias=-0.25, scale=-0.25)
            act(v("relj"), v("kio", 0, 144), AF.Identity, bias=c("col", 9))
            act(v("a32"), v("relj"), AF.Abs, bias=0.5)
            act(v("b32"), v("relj"), AF.Abs)
            act(v("i32"), IB, AF.Identity)
            act(v("hb"), IB, AF.Identity, scale=0.5)
            act(v("Z"), v("a32"), AF.Relu, bias=1.5, scale=-1.0)
            act(v("U"), v("b32"), AF.Relu, bias=1.0, scale=-1.0)
            ts(v("uu", 0, ROT), v("tI", K - ROT, K), 0.5, ALU.mult, c("col", 3), ALU.add)
            ts(v("uu", ROT, HK), v("tI", HK, K - ROT), 0.5, ALU.mult, c("col", 3), ALU.add)
        else:
            x_low(Xc, v("B6"), 0, 512)
            gat("A", ve(Xc, M), v("B6", 0, E))
            x_up(Xc, E, 2 * E)
            swap("aX%d" % (r - 1), ve(Xc, E), ve(Xc, M), ve(Xc, V), ve(Xc, ext_last(rank)), ve(Xc, ext_last(rank - 1)))
            gat("A", ve(Xc, M + E), v("B6", E, 2 * E))
            for a, b, bank in ((512, 1024, "B4"), (1024, 1536, "B2"), (1536, M, "B3")):
                x_low(Xc, v(bank, 0, b - a), a, b)
        ts(v("par", 96, 97 + C), v("B7", 16, 17 + C), -896.25, ALU.add)
        act(v("par", 112, 113 + C), v("B7", 16, 17 + C), AF.Identity, bias=c("col", 11 if last else 10))
        for b in range(1, C + 1):
            ts(v("te", HK * b, HK * b + HK), v("uu"), c("par", 96 + b), ALU.is_gt, c("par", 15 + b), ALU.mult)
        mm(v("B7", 64, 176), I16, v("uu"), True)
        for b in range(1, C + 1):
            mm(v("B7", 64, 176), I16, v("te", HK * b, HK * b + HK), False, b == C)
        ts(v("evI"), v("B7", 64, 176), -0.5, ALU.add)
        ts(v("evJ"), v("evI"), 1, ALU.bitwise_and)
        tt(v("cL", 0, ROT), v("cV", K - ROT, K), v("cA", K - ROT, K), ALU.add)
        tt(v("cL", ROT, 114), v("cV", HK, HK + 96), v("cA", HK, HK + 96), ALU.add)
        ts(v("oL", 0, HK), v("cL", 0, HK), -63.75, ALU.add)
        tt(v("cU", 0, ROT), v("cV", HK - ROT, HK), v("cA", HK - ROT, HK), ALU.add)
        tt(v("cU", ROT, 114), v("cV", 0, 96), v("cA", 0, 96), ALU.add)
        ts(v("oU", 0, 114), v("cU", 0, 114), -63.75, ALU.add)
        mm(v("B0", 0, HK), w("band", 0), v("cL", 0, HK), True)
        mm(v("B0", 0, HK), w("band", 128), v("cL", 1, HK + 1), False, True)
        if not last:
            dma("S", [(row("winA", 0, 0, WID), v("zero")), (row("winV", 0, 0, WID), v("zero"))])
        if r > 0:
            x_up(Xc, 0, E)
            for a, b, bank in ((512, 1024, "B4"), (1024, 1536, "B2"), (1536, M, "B3")):
                gat("A", v(Xc, M + a, M + b), v(bank, 0, b - a))
                x_up(Xc, a, b)
        lag[0] = 60
        for b in range(1, C):
            act(blk("mo", b), v("kio", 0, K) if last else v("tI"), AF.Sign, bias=c("par", 112 + b), scale=-1.0 if last else -0.5)
        for b in range(1, C):
            mm(v("B7", 256, 256 + K), v("hb"), blk("mo", b), b == 1, b == C - 1)
        act(v("so"), v("B7", 256, 256 + K), AF.Identity, bias=(C + 1) / 2.0)
        lag[0] = 0

        def low_names(a, b):
            gat("A", v("nl", 16 * a, 16 * b), ind(Nc, "oL", a, b, n))

        def check(a, b):
            tt(v("eq", 16 * a, 16 * b), ind("hint" if r == 0 else Gc, "oU", a, b, n), v("nl", 16 * a, 16 * b), ALU.is_equal)

        def mend(bank, bank2, a, b, piece):
            for i in range(16):
                mm(v(bank, a, b), w("Z" if i else "U", 16 - i), v("eq", 16 * a + i, 16 * b, 16), i == 0)
            e = min(b, HK - 1)
            mm(v(bank, a, e), w("U", 1), v("eq", 16 * a + 16, 16 * e + 1, 16), False, e == b)
            if e < b:
                mm(v(bank, e, b), w("U", 1), v("eq", 0, 1), False, True)
            p0, p1 = piece
            mm(v(bank2, p0, p1), v("i32"), v("cL", p0, p1), True)
            ts(v("fl", a, b), v(bank, a, b), 0.5, ALU.is_gt)
            tt(v("pp", a, b), v("fl", a, b), v("Dp", a, b), ALU.mult)
            if b == HK:
                cp(v("pp", 112, 114), v("pp", 0, 2))
            mm(v(bank2, p0, p1), w("band", 256), v("pp", p0, p1))
            mm(v(bank2, p0, p1), w("band", 384), v("pp", p0 - 1, p1 - 1), False, True)
            ts(v("o2", p0, p1), v(bank2, p0, p1), -63.75, ALU.add)

        def kc(a):
            return 16 * (a - 2)

        def uppers(a, b):
            gat("A", v(Xn, kc(a), kc(b)), ind(Xc, "oU", a, b, n))

        def diff(a, b):
            tt(v(Xn, M + kc(a), M + kc(b)), ind(Xc, "o2", a, b, n), v(Xn, kc(a), kc(b)), ALU.subtract)

        def greater(a, b):
            ts(v("gs", a, b), v(Xn, M + a, M + b), 0.5, ALU.is_gt)

        def sign(a, b, eng):
            if eng == "V":
                ts(v("gs", M + kc(a), M + kc(b)), v(Xn, M + kc(a), M + kc(b)), 1.0, ALU.min, -1.0, ALU.max)
            else:
                act(v("gs", M + kc(a), M + kc(b)), v(Xn, M + kc(a), M + kc(b)), AF.Sign)

        def wins_list(bank, a, b, o):
            for i in range(16):
                mm(v(bank, o, o + b - a), w("U", 16 - i), v("gs", M + kc(a) + i, M + kc(b), 16), i == 0, i == 15)

        def wins(i, a, b, name, bank, start=False, stop=False):
            t = K * i + a
            o = t + E if t < 1536 else t - 1536
            mm(v(bank, a, b), w("U", 8 - i) if name == "Yl" else w(name, 16 - i), v("gs", M + o, M + o + b - a), start, stop)

        def hist(out, offs, a, b):
            gat("A", out, ind(Gc, offs, a, b, n))

        def upper_ends():
            hist(v(Gn, 0, 512), "oU", *PE_)
            swap("aG%d" % r, ve(Gn, E), ve(Gn, 0), ve("pland", pl), ve(Gn, ext_last(rank)), ve(Gn, ext_last(rank - 1)))

        for a, b in CP:
            low_names(a, b)
        if r == 0:
            upper_ends()
        for piece in (PE_, PM1, PM2):
            uppers(*piece)
        for a, b in CP:
            check(a, b)
            if b == 36:
                tt(v("Dp"), v("B0", 0, HK), v("evJ"), ALU.mult)
            if a == 36:
                mend("B1", "B2", 0, 34, PE_)
            if a == 74:
                mend("B3", "B4", 34, 72, PM1)
        if r == 1:
            dma("S", [(row(Gc, rho, 0, n), row(Nc, 0, 0, n))])
        diff(*PE_)
        sign(*PE_, "V")
        if not last:
            wins_list("B7", 2, 34, 0)
        mend("B5", "B6", 72, HK, PM2)
        if not last:
            sn = "s%d" % (r + 1)
            diff(34, 54)
            act(v("cl", 96, HK), v("B7", 0, 16), AF.Sign)
            act(v("cl", 0, 16), v("B7", 16, 32), AF.Sign)
            if hasr:
                tt(v("sx", 16, 32), v("so", K - 16, K), v("cl", 96, HK), ALU.add)
            if hasl:
                tt(v("sx", 0, 16), v("so", 0, 16), v("cl", 0, 16), ALU.subtract)
            swap("aS%d" % r, v("sx", 0, 16), v("sx", 16, 32), v(sn, 0, 16), v(sn, K - 16, K))
            diff(54, 72)
            sign(*PM1, "A")
            wins_list("B0", 34, 72, 16)
            diff(72, 94)
            sign(72, 94, "A")
            diff(94, 114)
            sign(94, 114, "V")
            wins_list("B0", 72, 114, 54)
            ts(v("cl", 16, 96), v("B0", 16, 96), 1.0, ALU.min, -1.0, ALU.max)
            tt(v(sn, lo // 16, HK), v("so", lo // 16, HK), v("cl", lo // 16, HK), ALU.subtract)
            tt(v(sn, HK, hi // 16), v("so", HK, hi // 16), v("cl", 0, hi // 16 - HK), ALU.add)
            if r == 0:
                ts(v("h16"), v("rel"), 0.0, ALU.is_equal, 0.5, ALU.mult)
                lag[0] = 300
                tt(v("Y", 8, 144), v("U", 0, 136), v("U", 8, 144), ALU.add)
                lag[0] = 0
            if r == 1:
                upper_ends()
            hist(v(Gn, M, M + 512), "o2", *PE_)
            swap("aP%d" % r, ve(Gn, M + E), ve(Gn, M), ve(Gn, V), ve("pland", pl + E))
            if r == 0:
                for s in SHIFTS:
                    pick(shift(s), v("blk1"), ALU.is_equal, 0.0, -s)
            lag[0] = 60
            for a in range(0, M, 448):
                greater(a, a + 448)
            lag[0] = 0
            for offs, o in (("o2", M), ("oU", 0)):
                for a, b in ((34, 74), (74, 114)):
                    hist(v(Gn, o + kc(a), o + kc(b)), offs, a, b)
            dma("S", [(row(Nn, 0, 0, wid), row(Gn, rho, 0, wid))])
            fix = [(row(Gn, rho, 0, M), row(Nn, 0, M, V)), (row(Gn, rho, M, V), row(Nn, 0, 0, M))]
            if hasl:
                fix.append((row(Gn, rho, V, V + E), row("pland", rho, pl, pl + E)))
            if hasr:
                fix.append((row(Gn, rho, ext_last(rank), wid), row("pland", rho, pl + E, pl + 2 * E)))
            dma("S", [(row(Nn, j, 0, wid), row(Nn, 0, 0, wid)) for j in range(1, 16)])
            dma("S", fix)
        else:
            def names(eng, out, offs, a, b):
                gat(eng, out, ind(Nc, offs, a, b, n))

            def boards(bank, a, b):
                greater(a, b)
                tt(v("eq", a, b), v(Xn, a, b), v("gs", a, b), ALU.add)
                px = v(bank, 0, b - a)
                mm(px, IB, v(Xn, M + a, M + b), True)
                mm(px, v("ineg"), v("gs", M + a, M + b))
                mm(px, IB, v("eq", a, b), False, True)
                gat("A", v("xo", a, b), px)

            def middle(bank, a, b):
                boards(bank, a, b)
                dma("S", [(v("yx", a - E, b - E), v("eq", a, b)), (v("yx", M + a - E, M + b - E), v("xo", a, b))])

            yf = "Yl" if hasl else "Y"
            yl = "U" if hasr else "Y"
            wins(0, 0, K, "U", "B7", True)
            wins(1, 0, 32, "U", "B7")
            wins(6, 192, K, "Yl", "B7")
            wins(7, 0, K, "Yl", "B7", False, True)
            act(v("cl"), v("B7", 0, K), AF.Sign, scale=c("col", 8))
            tt(v("sE"), v("cl"), v("so"), ALU.add)
            swap("aS2", v("sE"), v("sE"), v("sinL"), v("sinR"))
            names("A", ve(Gn, V - E), "o2", 2, 18)
            names("A", ve(Gn, 0), "oU", 18, 34)
            swap("aN", ve(Gn, 0), ve(Gn, V - E), ve("nland", 0), ve("nland", E))
            boards("B2", 0, 512)
            swap("aX2", ve("eq", E), ve("xo", 0), ve("xland", 0), ve("xland", E))
            outs = [(ve("yx", 1536), ve("eq", 0)), (ve("yx", M), ve("xo", E))]
            if not hasl:
                outs.append((ve("yx", 0), ve("eq", E)))
            if not hasr:
                outs.append((ve("yx", V - E), ve("xo", 0)))
            dma("S", outs)
            diff(*PM1)
            sign(*PM1, "A")
            diff(72, 94)
            middle("B3", 512, 1024)
            sign(72, 94, "V")
            diff(94, 114)
            ends = []
            if hasl:
                ends += [(ve("yn", 0), row("nland", 0, 0, E)), (ve("yx", 0), ve("xland", 0))]
            if hasr:
                ends += [(ve("yn", V - E), row("nland", 0, E, 2 * E)), (ve("yx", V - E), ve("xland", E))]
            dma("S", ends)
            sign(94, 114, "V")
            middle("B4", 1024, 1472)
            middle("B5", 1472, M)
            mm(v("B1", 0, K), w("dk", 128), v("so"), True)
            if hasl:
                mm(v("B1", 0, 32), w("dn", 0), v("so", 0, 32))
            if hasr:
                mm(v("B1", 192, K), w("dn", 128), v("so", 192, K))
            from_ends("sinL", "sinR")
            wins(0, 0, K, yf, "B0", True)
            wins(1, 0, 32, yf, "B0")
            wins(6, 192, K, yl, "B0")
            wins(7, 0, K, yl, "B0")
            wins(1, 32, K, "Y", "B0")
            for i in (2, 3, 4, 5):
                wins(i, 0, K, "Y", "B0")
            wins(6, 0, 192, "Y", "B0", False, True)
            act(v("cl"), v("B0", 0, K), AF.Sign, scale=c("col", 8))
            tt(v("sf"), v("B1", 0, K), v("cl"), ALU.add)
            dma("S", [(v("ys"), v("sf"))])
            names("A", ve(Gn, 1536), "oU", 2, 18)
            for a, b in ((34, 60), (60, 88), (88, 114)):
                names("A", v(Gn, 16 * (a - ROT), 16 * (b - ROT)), "oU", a, b)
            dma("A", [(v("yn", lo, M), row(Gn, 0, lo, M))])
            names("V", v(Gn, M, 16 * (NS - ROT) + M), "o2", 18, NS)
            names("A", v(Gn, 16 * (NS - ROT) + M, V - E), "o2", NS, 114)
            dma("A", [(v("yn", M, hi), row(Gn, 0, M, hi))])
    emit(g, T, Q, arrange(ops))


def meets(a, b):
    for n1, l1, h1, r1 in a:
        for n2, l2, h2, r2 in b:
            if n1 == n2 and l1 < h2 and l2 < h1 and (r1 is None or r2 is None or r1 == r2):
                return True
    return False


def ordered(o, op):
    if o["eng"] == "P" and op["eng"] == "P":
        return bool(op["bank"] & o["bank"])
    return (meets(op["R"], o["W"]) or meets(op["W"], o["W"]) or meets(op["W"], o["R"])
            or (o["eng"] != op["eng"] and bool(op["bank"] & o["bank"])))


def arrange(ops):
    n = len(ops)
    by, sent, before, todo = {}, {}, {}, {}
    for k, op in enumerate(ops):
        op["names"] = set(x[0] for x in op["R"] + op["W"])
        op["bank"] = set(x for x in op["names"] if SCRATCH.get(x, ("",))[0] == "psum")
        cand = set()
        for x in op["names"]:
            cand.update(by.get(x, ()))
        dep = [j for j in cand if ordered(ops[j], op)]
        soft = [before[op["eng"]]] if (op["eng"] in ("S", "G") or op["kind"] == "d") and op["eng"] in before else []
        before[op["eng"]] = k
        if "pair" in op:
            sent[op["pair"]] = k
        if op["kind"] == "r":
            dep.append(sent[op["sem"]])
        for x in op["names"]:
            by.setdefault(x, []).append(k)
        op["nxt"], op["behind"] = [], []
        for j in dep:
            ops[j]["nxt"].append(k)
        for j in soft:
            ops[j]["behind"].append(k)
        cst = op["cost"]
        op["hold"], op["span"] = (cst[0], sum(cst)) if op["kind"] == "d" else (0.0, 0.4) if op["kind"] == "r" else (cst, cst)
        op["open"], op["known"] = set(dep) | set(soft), 0.0
        todo.setdefault(op["eng"], []).append(k)
    for k in range(n - 1, -1, -1):
        ops[k]["key"] = min([ops[k]["key"]] + [ops[j]["key"] - 0.01 for j in ops[k]["nxt"] + ops[k]["behind"]])
    for mine in todo.values():
        mine.sort(key=lambda k: (ops[k]["key"], k))
    free = {e: 0.0 for e in todo}
    wire, first, out = 0.0, True, []
    while len(out) < n:
        memo = {}

        def ready(k, depth):
            if k not in memo:
                op = ops[k]
                t = max(free[op["eng"]], op["known"])
                if op["open"]:
                    j = max(op["open"])
                    t = max(t, ready(j, depth + 1) + ops[j]["span"] + WAKE) if depth < DEPTH else t + 2.0
                memo[k] = t
            return memo[k]

        best = None
        for e, mine in todo.items():
            bound = 1e9
            for k in mine[:AHEAD.get(e, 4)]:
                t = ready(k, 0)
                if not ops[k]["open"] and t + ops[k]["hold"] <= bound + SLACK and (best is None or (t, ops[k]["key"]) < best[:2]):
                    best = (t, ops[k]["key"], k)
                bound = min(bound, t)
                if bound + SLACK <= free[e] + 0.03:
                    break
        at, _key, k = best
        op = ops[k]
        todo[op["eng"]].remove(k)
        out.append(k)
        hold = op["hold"]
        if "pair" in op and first:
            first = False
            hold += 2.5
        if op["kind"] != "r":
            free[op["eng"]] = at + hold
        if op["kind"] == "d":
            wire = max(wire, at + hold + op["cost"][1] / 2) + op["cost"][2]
            end = wire + op["cost"][1] / 2
        else:
            end = at + op["span"]
        for j in op["nxt"]:
            ops[j]["open"].discard(k)
            ops[j]["known"] = max(ops[j]["known"], end + (0.0 if op["eng"] == "P" and ops[j]["eng"] == "P" else WAKE))
        for j in op["behind"]:
            ops[j]["open"].discard(k)
            ops[j]["known"] = max(ops[j]["known"], at + hold)
    return [ops[k] for k in out]


def emit(g, T, Q, ops):
    know = {e: {} for e in Q}
    pos = {e: 0 for e in Q}
    nd = 0
    for k, op in enumerate(ops):
        e = op["eng"]
        if op["kind"] == "r":
            op["tok"], op["clock"], op["waits"] = (op["sem"], 1), {op["sem"]: 1}, []
            continue
        waits = []
        for j in range(k - 1, -1, -1):
            o = ops[j]
            if know[e].get(o["tok"][0], 0) >= o["tok"][1] or not (op["names"] & o["names"]):
                continue
            if o["eng"] == "P" and e == "P":
                continue
            if ordered(o, op):
                waits.append(j)
                o["seen"] = True
                for t, x in o["clock"].items():
                    if know[e].get(t, 0) < x:
                        know[e][t] = x
        op["waits"] = waits
        if op["kind"] == "c":
            pos[e] += 1
            op["tok"] = ("e" + e, pos[e])
        else:
            op["sem"] = "d%d" % nd
            nd += 1
            op["tok"] = (op["sem"], 1)
        op["clock"] = dict(know[e])
        op["clock"][op["tok"][0]] = op["tok"][1]
    count = {e: 0 for e in Q}
    for op in ops:
        e = op["eng"]
        if op["kind"] == "r":
            continue
        for j in op["waits"]:
            o = ops[j]
            if o["kind"] == "c":
                Q[e].wait_ge(T.sem[o["tok"][0]], o["val"])
            else:
                Q[e].wait_ge(T.sem[o["sem"]], o["n"])
        if op["kind"] == "c":
            ins = op["fn"]()
            if op.get("seen"):
                count[e] += 1
                op["val"] = count[e]
                ins.then_inc(T.sem["e" + e], 1)
        else:
            op["fn"](T.sem[op["sem"]])
    for op in ops:
        if op["kind"] != "c" and not op.get("seen"):
            g.wait_ge(T.sem[op["sem"]], op["n"])
